import numpy as np
import ml_dtypes


def mxq(x, axis, fmt="e4m3"):
    dtype, down = {"e4m3": (ml_dtypes.float8_e4m3fn, 7), "e5m2": (ml_dtypes.float8_e5m2, 14)}[fmt]
    v = np.moveaxis(np.asarray(x, np.float32).astype(ml_dtypes.bfloat16).astype(np.float64), axis, -1)
    blocks = v.reshape(v.shape[:-1] + (-1, 32))
    amax = np.abs(blocks).max(-1, keepdims=True)
    byte = np.maximum(np.where(amax > 0, np.frexp(amax)[1] - 1 + 127, 0) - down, 1)
    scale = np.exp2(byte - 127.0)
    codes = (blocks / scale).astype(np.float32).astype(dtype).astype(np.float64)
    return np.moveaxis((codes * scale).reshape(v.shape), -1, axis)


WIDE = False


def mx_kscale(k):
    if not WIDE:
        return np.ones(k)
    levels = np.array([10, -10, 5, -5, 0])
    if k % 512:
        return np.exp2(np.random.permutation(np.resize(levels, k // 32))).repeat(32)
    a = np.empty((k // 512, 16))
    for p in range(k // 512):
        a[p, :8] = np.random.permutation(np.resize(levels, 8))
        for g in range(8):
            far = levels[np.abs(levels - a[p, g]) >= 10]
            a[p, g + 8] = far[np.random.randint(len(far))]
    return np.exp2(a.ravel()).repeat(32)


def f64(x):
    return np.asarray(x).astype(np.float64)


def striped(idx):
    return np.tile(idx.reshape(-1, 16).T, (8, 1)).astype(np.uint16)


def unstriped(offs):
    return offs[:16].T.reshape(-1).astype(np.int64)


def relu2(v):
    return np.maximum(v, 0.0) ** 2


K, T, E, C, H, N = 1536, 1280, 6, 128, 512, 128


def by_expert(wq, xq):
    return np.concatenate([wq[e].T @ xq[:, e * C:(e + 1) * C] for e in range(E)], axis=1)


def setup_inputs():
    n = np.random.standard_normal
    s = mx_kscale(K)[:, None]
    u = mx_kscale(H)
    return {
        "xT": (n((K, T)) * s).astype(np.float32),
        "xr": n((N, T)).astype(np.float32),
        "w1": (n((E, K, H)) / np.sqrt(K) / s[None] * u[None, None, :]).astype(np.float32),
        "w2": (n((E, H, N)) / np.sqrt(H) / u[None, :, None] ** 2).astype(np.float32),
        "gate": np.tile(np.random.uniform(0.2, 1.0, E * C), (N, 1)).astype(np.float32),
        "offs": striped(np.random.permutation(T)[:E * C]),
    }


def reference(xT, xr, w1, w2, gate, offs):
    idx = unstriped(offs)
    xq = mxq(f64(xT)[:, idx], 0, "e4m3")
    h = relu2(by_expert(mxq(f64(w1), 1, "e4m3"), xq))
    y = by_expert(mxq(f64(w2), 1, "e4m3"), mxq(h, 0, "e4m3"))
    out = f64(xr).copy()
    out[:, idx] += f64(gate) * y
    return out

@@ -1,0 +1,265 @@
+from contextlib import ExitStack
+
+import concourse.mybir as mybir
+
+K, T, E, C, H, N = 1536, 1280, 6, 128, 512, 128
+S = E * C
+FLOPS = 2 * S * (K * H + H * N)
+
+F32 = mybir.dt.float32
+BF16 = mybir.dt.bfloat16
+U32 = mybir.dt.uint32
+U16 = mybir.dt.uint16
+U8 = mybir.dt.uint8
+FP8X4 = mybir.dt.float8_e4m3fn_x4
+COPY = mybir.ActivationFunctionType.Copy
+RELU = mybir.ActivationFunctionType.Relu
+SQUARE = mybir.ActivationFunctionType.Square
+MULT = mybir.AluOpType.mult
+ADD = mybir.AluOpType.add
+
+P = 128
+PACK = 4
+K_PASS = P * PACK
+PASSES = K // K_PASS
+TILES = H // P
+
+X_SCALAR = 512
+W_VECTOR = 56
+X_CHUNKS = ((512, 1024), (1024, 1280), (0, 512))
+W2_CHUNKS = {("w2", 0, 5): ((0, 512), (512, 640)), ("w2", 5, 6): ((640, 768),)}
+SCATTERS = {1: (0, 256), 3: (256, 448), 4: (448, 608), 5: (608, 768)}
+AHEAD = 6
+OUT_PIECES = ((0, 448), (448, 832), (832, 1088), (1088, 1280))
+
+
+def tile_moe_res_mlp_relu2_kernel(tc, xT, xr, w1, w2, gate, offs, out):
+    nc = tc.nc
+    with ExitStack() as ctx:
+        held = ctx.enter_context(tc.tile_pool(name="held", bufs=1))
+        xraws = ctx.enter_context(tc.tile_pool(name="xraws", bufs=3))
+        wraws = ctx.enter_context(tc.tile_pool(name="wraws", bufs=6))
+        xgrps = ctx.enter_context(tc.tile_pool(name="xgrps", bufs=2))
+        wgrps = ctx.enter_context(tc.tile_pool(name="wgrps", bufs=3))
+        wcods = ctx.enter_context(tc.tile_pool(name="wcods", bufs=6))
+        hids = ctx.enter_context(tc.tile_pool(name="hids", bufs=2))
+        psum = ctx.enter_context(tc.psum_pool(name="psum", bufs=1))
+        ypsum = ctx.enter_context(tc.psum_pool(name="ypsum", bufs=2))
+
+        lists = held.tile([P, S // 16], U16, name="lists")
+        planes = held.tile([P, T], U8, name="planes", align_bytes=64)
+        nc.gpsimd.memset(planes[:], 0)
+        window = held.tile([P, T], F32, name="window")
+        nc.gpsimd.memset(window[:], 0.0)
+
+        words = [held.tile([P, T], U32, name=f"words{s}", align_bytes=64) for s in range(PASSES)]
+        slot_words = [held.tile([P, S], U32, name=f"slot_words{s}", align_bytes=64) for s in range(PASSES)]
+        slot_planes = held.tile([P, S], U8, name="slot_planes", align_bytes=64)
+        w2_grp = held.tile([P, E * N * PACK], BF16, name="w2_grp", align_bytes=64)
+        w2_codes = held.tile([P, E * N], U32, name="w2_codes", align_bytes=64)
+        w2_scales = held.tile([P, E * N], U8, name="w2_scales", align_bytes=64)
+        gates = held.tile([P, S], F32, name="gates")
+        y_all = held.tile([P, S], F32, name="y_all")
+        result = held.tile([P, T], F32, name="result")
+
+        raw, grp, codes, scales, acc, relu, hid, y_sum = {}, {}, {}, {}, {}, {}, {}, {}
+
+        def load(item):
+            kind = item[0]
+            queue = nc.scalar if kind == "w" and item[1] > 1 and sum(item[1:]) % 2 == 0 else nc.sync
+            if kind == "x":
+                s = item[1]
+                t = xraws.tile([P, PACK, T], F32, name="x_raw")
+                queue.dma_start(out=t[:], in_=xT[s * K_PASS : (s + 1) * K_PASS, :].rearrange("(p j) t -> p j t", j=PACK))
+                raw[item] = t
+                if s == 0:
+                    nc.sync.dma_start(lists[:], offs)
+            elif kind == "w":
+                e, s = item[1], item[2]
+                t = wraws.tile([P, PACK * H], F32, name="w_raw")
+                queue.dma_start(out=t[:], in_=w1[e, s * K_PASS : (s + 1) * K_PASS, :].rearrange("(p j) i -> p (j i)", j=PACK))
+                raw[item] = t
+            elif kind == "w2":
+                a, b = item[1:]
+                if a:
+                    t = wraws.tile([P, b - a, PACK * N], F32, name="w_raw")
+                else:
+                    t = held.tile([P, b - a, PACK * N], F32, name="w2_raw")
+                raw[item] = t
+                queue.dma_start(out=t[:], in_=w2[a:b].rearrange("e (p j) n -> p e (j n)", j=PACK))
+            elif kind == "gate":
+                queue.dma_start(out=gates[:], in_=gate)
+            else:
+                t = wraws.tile([P, T], F32, name="w_raw")
+                raw[item] = t
+                queue.dma_start(out=t[:], in_=xr)
+
+        def cast(item):
+            kind = item[0]
+            if kind == "x":
+                g = xgrps.tile([P, T, PACK], BF16, name="x_grp", align_bytes=64)
+                grp[item] = g
+                dst = g[:].rearrange("p (c i) t -> p c t i", i=4)
+                src = raw[item][:].rearrange("p t (c i) -> p c t i", i=4)
+                nc.scalar.activation(dst[:, : X_SCALAR // 4], src[:, : X_SCALAR // 4], COPY)
+                nc.vector.tensor_copy(dst[:, X_SCALAR // 4 :], src[:, X_SCALAR // 4 :])
+            elif kind == "w":
+                g = wgrps.tile([P, H * PACK], BF16, name="w_grp", align_bytes=64)
+                grp[item] = g
+                dst = g[:].rearrange("p (t m j) -> p m j t", t=TILES, j=PACK)
+                src = raw[item][:].rearrange("p (j m t) -> p m j t", t=TILES, j=PACK)
+                cut = (88 if item[1:] == (E - 1, PASSES - 1) else W_VECTOR) if item[1] else 128 * (item[2] == 0)
+                if cut:
+                    nc.vector.tensor_copy(dst[:, :cut], src[:, :cut])
+                if cut < 128:
+                    nc.scalar.activation(dst[:, cut:], src[:, cut:], COPY)
+            elif kind == "w2":
+                a, b = item[1:]
+                for e in range(a, b):
+                    dst = w2_grp[:, e * N * PACK : (e + 1) * N * PACK].rearrange("p (c i j) -> p c j i", i=4, j=PACK)
+                    src = raw[item][:, e - a, :].rearrange("p (j c i) -> p c j i", i=4, j=PACK)
+                    nc.scalar.activation(dst, src, COPY)
+
+        def quantise(item):
+            kind = item[0]
+            if kind == "x":
+                s = item[1]
+                flat = grp[item][:].rearrange("p n t -> p (n t)")
+                for a, b in X_CHUNKS:
+                    nc.vector.quantize_mx(
+                        out=words[s][:, a:b].bitcast(FP8X4),
+                        scales=planes[4 * s : P, a:b],
+                        in_=flat[:, PACK * a : PACK * b],
+                    )
+            elif kind == "w":
+                c = wcods.tile([P, H], U32, name="w_codes", align_bytes=64)
+                z = wcods.tile([P, H], U8, name="w_scales", align_bytes=64)
+                width = P if item[1:] == (E - 1, PASSES - 1) else H
+                for a in range(0, H, width):
+                    b = a + width
+                    nc.vector.quantize_mx(out=c[:, a:b].bitcast(FP8X4), scales=z[:, a:b], in_=grp[item][:, PACK * a : PACK * b])
+                codes[item], scales[item] = c, z
+            elif kind == "w2":
+                for a, b in W2_CHUNKS[item]:
+                    nc.vector.quantize_mx(
+                        out=w2_codes[:, a:b].bitcast(FP8X4),
+                        scales=w2_scales[:, a:b],
+                        in_=w2_grp[:, PACK * a : PACK * b],
+                    )
+
+        def gather(s):
+            nc.vector.tensor_copy(slot_words[s][:], words[s][:].indirect(lists[:]))
+            if s == PASSES - 1:
+                nc.vector.tensor_copy(slot_planes[:], planes[:].indirect(lists[:]))
+
+        def multiply(e, s):
+            if e < E - 1:
+                if s < PASSES - 1:
+                    return
+                sums = psum.tile([P, TILES, C], F32, name="sums", bufs=2)
+                acc[e] = [sums[:, t, :] for t in range(TILES)]
+                whole[e] = sums
+                order = [(t, k) for t in range(TILES) for k in range(PASSES)]
+            else:
+                if s == 0:
+                    tiles = [psum.tile([P, C], F32, name=f"last{t}") for t in range(TILES)]
+                    acc[e] = [tile[:] for tile in tiles]
+                order = [(t, s) for t in range(TILES)]
+            cols = slice(e * C, (e + 1) * C)
+            for t, k in order:
+                rows = slice(t * P, (t + 1) * P)
+                nc.tensor.matmul_mx(
+                    out=acc[e][t],
+                    lhsT=codes["w", e, k][:, rows].bitcast(FP8X4),
+                    lhsT_scale=scales["w", e, k][:, rows],
+                    rhs=slot_words[k][:, cols].bitcast(FP8X4),
+                    rhs_scale=slot_planes[4 * k : P, cols],
+                    start=(k == 0),
+                    stop=(k == PASSES - 1),
+                )
+
+        def rectify(e):
+            r = hids.tile([P, TILES, C], F32, name="relu_out")
+            if e < E - 1:
+                nc.scalar.activation(r[:], whole[e][:], RELU)
+            else:
+                for t in range(TILES):
+                    if t % 2:
+                        nc.vector.tensor_scalar_max(r[:, t, :], acc[e][t], 0.0)
+                    else:
+                        nc.scalar.activation(r[:, t, :], acc[e][t], RELU)
+            relu[e] = r
+
+        def square(e):
+            g = hids.tile([P, C, TILES], BF16, name="h_grp", align_bytes=64)
+            src = relu[e][:].rearrange("p t c -> p c t")
+            half = C // 2
+            nc.scalar.activation(g[:, :half, :], src[:, :half, :], SQUARE)
+            nc.vector.tensor_tensor(g[:, half:, :], src[:, half:, :], src[:, half:, :], MULT)
+            hid[e] = g
+
+        def second(e):
+            c = hids.tile([P, C], U32, name="h_codes", align_bytes=64)
+            z = hids.tile([P, C], U8, name="h_scales", align_bytes=64)
+            nc.vector.quantize_mx(out=c[:].bitcast(FP8X4), scales=z[:], in_=hid[e][:].rearrange("p c t -> p (c t)"))
+            y = ypsum.tile([P, C], F32, name="y")
+            cols = slice(e * N, (e + 1) * N)
+            nc.tensor.matmul_mx(
+                out=y[:],
+                lhsT=w2_codes[:, cols].bitcast(FP8X4),
+                lhsT_scale=w2_scales[:, cols],
+                rhs=c[:].bitcast(FP8X4),
+                rhs_scale=z[:],
+                start=True,
+                stop=True,
+            )
+            y_sum[e] = y
+
+        def collect(e):
+            if e < E - 1:
+                nc.scalar.activation(y_all[:, e * C : (e + 1) * C], y_sum[e][:], COPY)
+            else:
+                nc.vector.tensor_copy(y_all[:, e * C : (e + 1) * C], y_sum[e][:])
+
+        def scatter(e):
+            if e in SCATTERS:
+                a, b = SCATTERS[e]
+                nc.vector.tensor_tensor(window[:].indirect(lists[:, a // 16 : b // 16]), y_all[:, a:b], gates[:, a:b], MULT)
+
+        whole = {}
+        due = {}
+        items = []
+        items += [("w", 0, 0), ("x", 0), ("w2", 0, E - 1), ("x", 1), ("w", 0, 1), ("x", 2), ("w", 0, 2), ("gate",)]
+        items += [("w", e, s) for e in range(1, E) for s in range(PASSES)]
+        items += [("w2", E - 1, E), ("xr",)]
+
+        for item in items[:AHEAD]:
+            load(item)
+        waiting = []
+        stages = ((5, scatter), (4, collect), (3, second), (2, square), (1, rectify))
+        for i in range(len(items) + 6):
+            if i + AHEAD < len(items):
+                load(items[i + AHEAD])
+            for delay, stage in stages:
+                for e in range(E):
+                    if due.get(e) == i - delay:
+                        stage(e)
+            if 0 <= i - 1 < len(items):
+                item = items[i - 1]
+                quantise(item)
+                if item[0] == "x":
+                    gather(item[1])
+                if item[0] == "w":
+                    waiting.append(item)
+                if i > items.index(("x", PASSES - 1)):
+                    for w in waiting:
+                        multiply(w[1], w[2])
+                        if w[2] == PASSES - 1:
+                            due[w[1]] = i
+                    waiting = []
+            if i < len(items):
+                cast(items[i])
+
+        for a, b in OUT_PIECES:
+            nc.vector.tensor_tensor(result[:, a:b], window[:, a:b], raw["xr",][:, a:b], ADD)
+            nc.sync.dma_start(out=out[:, a:b], in_=result[:, a:b])

@@ -24,13 +24,15 @@ K_PASS = P * PACK
 PASSES = K // K_PASS
 TILES = H // P
 
-X_SCALAR = 512
-W_VECTOR = 56
-X_CHUNKS = ((512, 1024), (1024, 1280), (0, 512))
-W2_CHUNKS = {("w2", 0, 5): ((0, 512), (512, 640)), ("w2", 5, 6): ((640, 768),)}
-SCATTERS = {1: (0, 256), 3: (256, 448), 4: (448, 608), 5: (608, 768)}
-AHEAD = 6
+X_SCALAR = 896
+W_VECTOR = (40, 40, 64)
+W_VECTOR_LAST = (48, 64, 88)
+GATE_EARLY = (E - 2) * C
+X_CHUNKS = ((1024, 1280), (0, 512), (512, 1024))
+RING = 7
+AHEAD = 4
 OUT_PIECES = ((0, 448), (448, 832), (832, 1088), (1088, 1280))
+LAST = E - 1
 
 
 def tile_moe_res_mlp_relu2_kernel(tc, xT, xr, w1, w2, gate, offs, out):
@@ -38,7 +40,6 @@ def tile_moe_res_mlp_relu2_kernel(tc, xT, xr, w1, w2, gate, offs, out):
     with ExitStack() as ctx:
         held = ctx.enter_context(tc.tile_pool(name="held", bufs=1))
         xraws = ctx.enter_context(tc.tile_pool(name="xraws", bufs=3))
-        wraws = ctx.enter_context(tc.tile_pool(name="wraws", bufs=6))
         xgrps = ctx.enter_context(tc.tile_pool(name="xgrps", bufs=2))
         wgrps = ctx.enter_context(tc.tile_pool(name="wgrps", bufs=3))
         wcods = ctx.enter_context(tc.tile_pool(name="wcods", bufs=6))
@@ -48,9 +49,11 @@ def tile_moe_res_mlp_relu2_kernel(tc, xT, xr, w1, w2, gate, offs, out):
 
         lists = held.tile([P, S // 16], U16, name="lists")
         planes = held.tile([P, T], U8, name="planes", align_bytes=64)
-        nc.gpsimd.memset(planes[:], 0)
+        nc.vector.memset(planes[:], 0)
         window = held.tile([P, T], F32, name="window")
-        nc.gpsimd.memset(window[:], 0.0)
+        nc.vector.memset(window[:], 0.0)
+        zeros = held.tile([P, C], F32, name="zeros")
+        nc.vector.memset(zeros[:], 0.0)
 
         words = [held.tile([P, T], U32, name=f"words{s}", align_bytes=64) for s in range(PASSES)]
         slot_words = [held.tile([P, S], U32, name=f"slot_words{s}", align_bytes=64) for s in range(PASSES)]
@@ -58,102 +61,92 @@ def tile_moe_res_mlp_relu2_kernel(tc, xT, xr, w1, w2, gate, offs, out):
         w2_grp = held.tile([P, E * N * PACK], BF16, name="w2_grp", align_bytes=64)
         w2_codes = held.tile([P, E * N], U32, name="w2_codes", align_bytes=64)
         w2_scales = held.tile([P, E * N], U8, name="w2_scales", align_bytes=64)
-        gates = held.tile([P, S], F32, name="gates")
-        y_all = held.tile([P, S], F32, name="y_all")
+        gates = {a: held.tile([P, b - a], F32, name=f"gates{a}") for a, b in ((0, GATE_EARLY), (GATE_EARLY, S))}
         result = held.tile([P, T], F32, name="result")
+        last_relu = held.tile([P, TILES, C], F32, name="last_relu")
+        ring = [held.tile([P, PACK * H], F32, name=f"ring{r}", align_bytes=64) for r in range(RING)]
 
-        raw, grp, codes, scales, acc, relu, hid, y_sum = {}, {}, {}, {}, {}, {}, {}, {}
+        passes = [("w", e, s) for e in range(E) for s in range(PASSES)]
+        ringed = passes[: LAST * PASSES] + [("w2", LAST - 1, LAST)] + passes[LAST * PASSES :] + [("w2", LAST, E), ("xr",)]
+        raw = {item: ring[i % RING] for i, item in enumerate(ringed)}
+        grp, codes, scales, acc, whole, relu, hid, y_sum, gated = {}, {}, {}, {}, {}, {}, {}, {}, {}
 
         def load(item):
             kind = item[0]
-            queue = nc.scalar if kind == "w" and item[1] > 1 and sum(item[1:]) % 2 == 0 else nc.sync
             if kind == "x":
                 s = item[1]
                 t = xraws.tile([P, PACK, T], F32, name="x_raw")
-                queue.dma_start(out=t[:], in_=xT[s * K_PASS : (s + 1) * K_PASS, :].rearrange("(p j) t -> p j t", j=PACK))
+                nc.sync.dma_start(out=t[:], in_=xT[s * K_PASS : (s + 1) * K_PASS, :].rearrange("(p j) t -> p j t", j=PACK))
                 raw[item] = t
                 if s == 0:
                     nc.sync.dma_start(lists[:], offs)
             elif kind == "w":
                 e, s = item[1], item[2]
-                t = wraws.tile([P, PACK * H], F32, name="w_raw")
-                queue.dma_start(out=t[:], in_=w1[e, s * K_PASS : (s + 1) * K_PASS, :].rearrange("(p j) i -> p (j i)", j=PACK))
-                raw[item] = t
+                nc.sync.dma_start(out=raw[item][:], in_=w1[e, s * K_PASS : (s + 1) * K_PASS, :].rearrange("(p j) i -> p (j i)", j=PACK))
             elif kind == "w2":
                 a, b = item[1:]
-                if a:
-                    t = wraws.tile([P, b - a, PACK * N], F32, name="w_raw")
-                else:
-                    t = held.tile([P, b - a, PACK * N], F32, name="w2_raw")
-                raw[item] = t
-                queue.dma_start(out=t[:], in_=w2[a:b].rearrange("e (p j) n -> p e (j n)", j=PACK))
+                if a == 0:
+                    raw[item] = xraws.tile([P, (b - a) * PACK * N], F32, name="x_raw")
+                dst = raw[item][:, : (b - a) * PACK * N].rearrange("p (e q) -> p e q", e=b - a)
+                nc.sync.dma_start(out=dst, in_=w2[a:b].rearrange("e (p j) n -> p e (j n)", j=PACK))
             elif kind == "gate":
-                queue.dma_start(out=gates[:], in_=gate)
-            else:
-                t = wraws.tile([P, T], F32, name="w_raw")
-                raw[item] = t
-                queue.dma_start(out=t[:], in_=xr)
-
-        def cast(item):
-            kind = item[0]
-            if kind == "x":
-                g = xgrps.tile([P, T, PACK], BF16, name="x_grp", align_bytes=64)
-                grp[item] = g
-                dst = g[:].rearrange("p (c i) t -> p c t i", i=4)
-                src = raw[item][:].rearrange("p t (c i) -> p c t i", i=4)
-                nc.scalar.activation(dst[:, : X_SCALAR // 4], src[:, : X_SCALAR // 4], COPY)
-                nc.vector.tensor_copy(dst[:, X_SCALAR // 4 :], src[:, X_SCALAR // 4 :])
-            elif kind == "w":
-                g = wgrps.tile([P, H * PACK], BF16, name="w_grp", align_bytes=64)
-                grp[item] = g
-                dst = g[:].rearrange("p (t m j) -> p m j t", t=TILES, j=PACK)
-                src = raw[item][:].rearrange("p (j m t) -> p m j t", t=TILES, j=PACK)
-                cut = (88 if item[1:] == (E - 1, PASSES - 1) else W_VECTOR) if item[1] else 128 * (item[2] == 0)
-                if cut:
-                    nc.vector.tensor_copy(dst[:, :cut], src[:, :cut])
-                if cut < 128:
-                    nc.scalar.activation(dst[:, cut:], src[:, cut:], COPY)
-            elif kind == "w2":
                 a, b = item[1:]
-                for e in range(a, b):
-                    dst = w2_grp[:, e * N * PACK : (e + 1) * N * PACK].rearrange("p (c i j) -> p c j i", i=4, j=PACK)
-                    src = raw[item][:, e - a, :].rearrange("p (j c i) -> p c j i", i=4, j=PACK)
-                    nc.scalar.activation(dst, src, COPY)
+                nc.sync.dma_start(out=gates[a][:], in_=gate[:, a:b])
+            else:
+                nc.sync.dma_start(out=raw[item][:, :T], in_=xr)
 
-        def quantise(item):
-            kind = item[0]
-            if kind == "x":
-                s = item[1]
-                flat = grp[item][:].rearrange("p n t -> p (n t)")
-                for a, b in X_CHUNKS:
-                    nc.vector.quantize_mx(
-                        out=words[s][:, a:b].bitcast(FP8X4),
-                        scales=planes[4 * s : P, a:b],
-                        in_=flat[:, PACK * a : PACK * b],
-                    )
-            elif kind == "w":
-                c = wcods.tile([P, H], U32, name="w_codes", align_bytes=64)
-                z = wcods.tile([P, H], U8, name="w_scales", align_bytes=64)
-                width = P if item[1:] == (E - 1, PASSES - 1) else H
-                for a in range(0, H, width):
-                    b = a + width
-                    nc.vector.quantize_mx(out=c[:, a:b].bitcast(FP8X4), scales=z[:, a:b], in_=grp[item][:, PACK * a : PACK * b])
-                codes[item], scales[item] = c, z
-            elif kind == "w2":
-                for a, b in W2_CHUNKS[item]:
-                    nc.vector.quantize_mx(
-                        out=w2_codes[:, a:b].bitcast(FP8X4),
-                        scales=w2_scales[:, a:b],
-                        in_=w2_grp[:, PACK * a : PACK * b],
-                    )
-
-        def gather(s):
+        def tokens(s):
+            g = xgrps.tile([P, T, PACK], BF16, name="x_grp", align_bytes=64)
+            dst = g[:].rearrange("p (c i) t -> p c t i", i=4)
+            src = raw["x", s][:].rearrange("p t (c i) -> p c t i", i=4)
+            for a, b in ((0, 512), (512, X_SCALAR)):
+                nc.scalar.activation(dst[:, a // 4 : b // 4], src[:, a // 4 : b // 4], COPY)
+            nc.vector.tensor_copy(dst[:, X_SCALAR // 4 :], src[:, X_SCALAR // 4 :])
+            flat = g[:].rearrange("p n t -> p (n t)")
+            for a, b in X_CHUNKS:
+                nc.vector.quantize_mx(
+                    out=words[s][:, a:b].bitcast(FP8X4),
+                    scales=planes[4 * s : P, a:b],
+                    in_=flat[:, PACK * a : PACK * b],
+                )
             nc.vector.tensor_copy(slot_words[s][:], words[s][:].indirect(lists[:]))
             if s == PASSES - 1:
                 nc.vector.tensor_copy(slot_planes[:], planes[:].indirect(lists[:]))
 
+        def cast(e, s):
+            g = wgrps.tile([P, H * PACK], BF16, name="w_grp", align_bytes=64)
+            grp[e, s] = g
+            dst = g[:].rearrange("p (t m j) -> p m j t", t=TILES, j=PACK)
+            src = raw["w", e, s][:].rearrange("p (j m t) -> p m j t", t=TILES, j=PACK)
+            cut = (W_VECTOR_LAST if e == LAST else W_VECTOR)[s] if e else P * (s == 0)
+            if cut:
+                nc.vector.tensor_copy(dst[:, :cut], src[:, :cut])
+            if cut < P:
+                nc.scalar.activation(dst[:, cut:], src[:, cut:], COPY)
+
+        def quantise(e, s):
+            c = wcods.tile([P, H], U32, name="w_codes", align_bytes=64)
+            z = wcods.tile([P, H], U8, name="w_scales", align_bytes=64)
+            width = P if (e, s) == (LAST, PASSES - 1) else H
+            for a in range(0, H, width):
+                b = a + width
+                nc.vector.quantize_mx(out=c[:, a:b].bitcast(FP8X4), scales=z[:, a:b], in_=grp[e, s][:, PACK * a : PACK * b])
+            codes[e, s], scales[e, s] = c, z
+
+        def second_weights(a, b, chunks):
+            for e in range(a, b):
+                dst = w2_grp[:, e * N * PACK : (e + 1) * N * PACK].rearrange("p (c i j) -> p c j i", i=4, j=PACK)
+                src = raw["w2", a, b][:, (e - a) * N * PACK : (e - a + 1) * N * PACK].rearrange("p (j c i) -> p c j i", i=4, j=PACK)
+                nc.scalar.activation(dst, src, COPY)
+            for lo, hi in chunks:
+                nc.vector.quantize_mx(
+                    out=w2_codes[:, lo:hi].bitcast(FP8X4),
+                    scales=w2_scales[:, lo:hi],
+                    in_=w2_grp[:, PACK * lo : PACK * hi],
+                )
+
         def multiply(e, s):
-            if e < E - 1:
+            if e < LAST:
                 if s < PASSES - 1:
                     return
                 sums = psum.tile([P, TILES, C], F32, name="sums", bufs=2)
@@ -170,38 +163,53 @@ def tile_moe_res_mlp_relu2_kernel(tc, xT, xr, w1, w2, gate, offs, out):
                 rows = slice(t * P, (t + 1) * P)
                 nc.tensor.matmul_mx(
                     out=acc[e][t],
-                    lhsT=codes["w", e, k][:, rows].bitcast(FP8X4),
-                    lhsT_scale=scales["w", e, k][:, rows],
+                    lhsT=codes[e, k][:, rows].bitcast(FP8X4),
+                    lhsT_scale=scales[e, k][:, rows],
                     rhs=slot_words[k][:, cols].bitcast(FP8X4),
                     rhs_scale=slot_planes[4 * k : P, cols],
                     start=(k == 0),
                     stop=(k == PASSES - 1),
                 )
 
-        def rectify(e):
-            r = hids.tile([P, TILES, C], F32, name="relu_out")
-            if e < E - 1:
-                nc.scalar.activation(r[:], whole[e][:], RELU)
+        def step_of(e, stage):
+            return (e + 1) * PASSES + stage + (e < LAST - 1)
+
+        def lent(e, stage):
+            return raw[passes[step_of(e, stage)]]
+
+        def hidden(e):
+            if e < LAST:
+                r = lent(e, 0)[:].rearrange("p (j h) -> p j h", j=PACK)[:, :, :C]
+                nc.scalar.activation(
+                    r.rearrange("p j (c t) -> p j c t", t=TILES),
+                    whole[e][:].rearrange("p t (j c) -> p j c t", j=PACK),
+                    RELU,
+                )
+                relu[e] = r
             else:
                 for t in range(TILES):
-                    if t % 2:
-                        nc.vector.tensor_scalar_max(r[:, t, :], acc[e][t], 0.0)
-                    else:
-                        nc.scalar.activation(r[:, t, :], acc[e][t], RELU)
-            relu[e] = r
+                    nc.scalar.activation(last_relu[:, t, :], acc[e][t], RELU)
 
         def square(e):
-            g = hids.tile([P, C, TILES], BF16, name="h_grp", align_bytes=64)
-            src = relu[e][:].rearrange("p t c -> p c t")
-            half = C // 2
-            nc.scalar.activation(g[:, :half, :], src[:, :half, :], SQUARE)
-            nc.vector.tensor_tensor(g[:, half:, :], src[:, half:, :], src[:, half:, :], MULT)
+            if e < LAST:
+                if e < LAST - 1:
+                    g = lent(e, 1)[:, : C * TILES // 2].bitcast(BF16)
+                else:
+                    g = hids.tile([P, C * TILES], BF16, name="h_grp", align_bytes=64)[:]
+                nc.vector.tensor_tensor(g.rearrange("p (j q) -> p j q", j=PACK), relu[e], relu[e], MULT)
+            else:
+                g = hids.tile([P, C * TILES], BF16, name="h_grp", align_bytes=64)[:]
+                src = last_relu[:].rearrange("p t c -> p c t")
+                dst = g.rearrange("p (c t) -> p c t", t=TILES)
+                half = C // 2
+                nc.scalar.activation(dst[:, :half, :], src[:, :half, :], SQUARE)
+                nc.vector.tensor_tensor(dst[:, half:, :], src[:, half:, :], src[:, half:, :], MULT)
             hid[e] = g
 
         def second(e):
             c = hids.tile([P, C], U32, name="h_codes", align_bytes=64)
             z = hids.tile([P, C], U8, name="h_scales", align_bytes=64)
-            nc.vector.quantize_mx(out=c[:].bitcast(FP8X4), scales=z[:], in_=hid[e][:].rearrange("p c t -> p (c t)"))
+            nc.vector.quantize_mx(out=c[:].bitcast(FP8X4), scales=z[:], in_=hid[e])
             y = ypsum.tile([P, C], F32, name="y")
             cols = slice(e * N, (e + 1) * N)
             nc.tensor.matmul_mx(
@@ -215,50 +223,56 @@ def tile_moe_res_mlp_relu2_kernel(tc, xT, xr, w1, w2, gate, offs, out):
             )
             y_sum[e] = y
 
-        def collect(e):
-            if e < E - 1:
-                nc.scalar.activation(y_all[:, e * C : (e + 1) * C], y_sum[e][:], COPY)
+        def weigh(e):
+            first = GATE_EARLY if e * C >= GATE_EARLY else 0
+            if e in (LAST - 2, LAST):
+                gated[e] = hids.tile([P, C], F32, name="gated")[:]
+            elif e == LAST - 1:
+                gated[e] = lent(e, 2)[:, PACK * H - C :]
             else:
-                nc.vector.tensor_copy(y_all[:, e * C : (e + 1) * C], y_sum[e][:])
+                gated[e] = lent(e, 2)[:, (PACK - 1) * H : (PACK - 1) * H + C]
+            nc.vector.tensor_tensor(gated[e], y_sum[e][:], gates[first][:, e * C - first : (e + 1) * C - first], MULT)
 
         def scatter(e):
-            if e in SCATTERS:
-                a, b = SCATTERS[e]
-                nc.vector.tensor_tensor(window[:].indirect(lists[:, a // 16 : b // 16]), y_all[:, a:b], gates[:, a:b], MULT)
+            columns = C // 16
+            nc.vector.tensor_tensor(window[:].indirect(lists[:, e * columns : (e + 1) * columns]), gated[e], zeros[:], ADD)
 
-        whole = {}
-        due = {}
-        items = []
-        items += [("w", 0, 0), ("x", 0), ("w2", 0, E - 1), ("x", 1), ("w", 0, 1), ("x", 2), ("w", 0, 2), ("gate",)]
-        items += [("w", e, s) for e in range(1, E) for s in range(PASSES)]
-        items += [("w2", E - 1, E), ("xr",)]
-
-        for item in items[:AHEAD]:
+        for s in range(PASSES):
+            load(("x", s))
+        for item in ringed[:PASSES] + [("w2", 0, LAST - 1), ("gate", 0, GATE_EARLY)] + ringed[PASSES:AHEAD]:
             load(item)
-        waiting = []
-        stages = ((5, scatter), (4, collect), (3, second), (2, square), (1, rectify))
-        for i in range(len(items) + 6):
-            if i + AHEAD < len(items):
-                load(items[i + AHEAD])
-            for delay, stage in stages:
-                for e in range(E):
-                    if due.get(e) == i - delay:
-                        stage(e)
-            if 0 <= i - 1 < len(items):
-                item = items[i - 1]
-                quantise(item)
-                if item[0] == "x":
-                    gather(item[1])
-                if item[0] == "w":
-                    waiting.append(item)
-                if i > items.index(("x", PASSES - 1)):
-                    for w in waiting:
-                        multiply(w[1], w[2])
-                        if w[2] == PASSES - 1:
-                            due[w[1]] = i
-                    waiting = []
-            if i < len(items):
-                cast(items[i])
+        for s in range(PASSES):
+            tokens(s)
+        loaded = AHEAD
+        for i in range(E * PASSES):
+            e, s = divmod(i, PASSES)
+            at = ringed.index(passes[i])
+            while loaded <= min(at + AHEAD, len(ringed) - 1):
+                load(ringed[loaded])
+                if ringed[loaded] == ("w", LAST, 0):
+                    load(("gate", GATE_EARLY, S))
+                loaded = loaded + 1
+            if i == LAST * PASSES:
+                second_weights(LAST - 1, LAST, ((512, 640),))
+            due = {stage: d for d in range(LAST) for stage in range(3) if step_of(d, stage) == i}
+            cast(e, s)
+            for stage, work in ((2, weigh), (2, scatter), (0, hidden), (1, square)):
+                if stage in due and not (stage == 2 and due[stage] == LAST - 1):
+                    work(due[stage])
+            quantise(e, s)
+            if 1 in due:
+                second(due[1])
+            multiply(e, s)
+            if i == PASSES - 1:
+                second_weights(0, LAST - 1, ((0, 512),))
+        weigh(LAST - 1)
+        second_weights(LAST, E, ((640, 768),))
+        scatter(LAST - 1)
+        hidden(LAST)
+        square(LAST)
+        second(LAST)
+        weigh(LAST)
+        scatter(LAST)
 
         for a, b in OUT_PIECES:
             nc.vector.tensor_tensor(result[:, a:b], window[:, a:b], raw["xr",][:, a:b], ADD)

@@ -1,6 +1,7 @@
 from contextlib import ExitStack
 
 import concourse.mybir as mybir
+from concourse.masks import make_identity
 
 K, T, E, C, H, N = 1536, 1280, 6, 128, 512, 128
 S = E * C
@@ -25,14 +26,13 @@ PASSES = K // K_PASS
 TILES = H // P
 
 X_SCALAR = 896
-W_VECTOR = (40, 40, 64)
-W_VECTOR_LAST = (48, 64, 88)
-GATE_EARLY = (E - 2) * C
+W_VECTOR = (56, 64, 88)
+W_VECTOR_LAST = (52, 44)
+W_VECTOR_LATE = 88
 X_CHUNKS = ((1024, 1280), (0, 512), (512, 1024))
-RING = 7
-AHEAD = 4
 OUT_PIECES = ((0, 448), (448, 832), (832, 1088), (1088, 1280))
 LAST = E - 1
+PAIRED = 2
 
 
 def tile_moe_res_mlp_relu2_kernel(tc, xT, xr, w1, w2, gate, offs, out):
@@ -61,14 +61,31 @@ def tile_moe_res_mlp_relu2_kernel(tc, xT, xr, w1, w2, gate, offs, out):
         w2_grp = held.tile([P, E * N * PACK], BF16, name="w2_grp", align_bytes=64)
         w2_codes = held.tile([P, E * N], U32, name="w2_codes", align_bytes=64)
         w2_scales = held.tile([P, E * N], U8, name="w2_scales", align_bytes=64)
-        gates = {a: held.tile([P, b - a], F32, name=f"gates{a}") for a, b in ((0, GATE_EARLY), (GATE_EARLY, S))}
+        gates = held.tile([P, S], F32, name="gates")
+        gate_rows = held.tile([P, C], F32, name="gate_rows")
+        nc.vector.memset(gate_rows[:], 0.0)
+        gate_cols = held.tile([P, E], F32, name="gate_cols")
+        identity = held.tile([P, P], F32, name="identity")
+        make_identity(nc, identity[:])
         result = held.tile([P, T], F32, name="result")
         last_relu = held.tile([P, TILES, C], F32, name="last_relu")
-        ring = [held.tile([P, PACK * H], F32, name=f"ring{r}", align_bytes=64) for r in range(RING)]
+        pairs = [held.tile([P, 2, PACK * H], F32, name=f"pair{r}", align_bytes=64) for r in range(3)]
+        singles = [held.tile([P, PACK * H], F32, name=f"single{r}", align_bytes=64) for r in range(2)]
+        seconds = [held.tile([P, PACK * N], F32, name=f"second{r}") for r in range(2)]
 
         passes = [("w", e, s) for e in range(E) for s in range(PASSES)]
-        ringed = passes[: LAST * PASSES] + [("w2", LAST - 1, LAST)] + passes[LAST * PASSES :] + [("w2", LAST, E), ("xr",)]
-        raw = {item: ring[i % RING] for i, item in enumerate(ringed)}
+        raw = {("xr",): pairs[0][:, 1, :]}
+        loads = [("pair", 0)]
+        raw[passes[0]], raw[passes[1]] = pairs[0][:, 0, :], pairs[0][:, 1, :]
+        for e in range(LAST):
+            i = e * PASSES + PASSES - 1
+            raw[passes[i]], raw[passes[i + 1]] = pairs[(e + 1) % 3][:, 0, :], pairs[(e + 1) % 3][:, 1, :]
+            raw[passes[i + 2]] = singles[e % 2][:]
+            loads.extend([("pair", i), ("w2", e, e + 1), passes[i + 2]])
+        raw[passes[-1]] = pairs[0][:, 0, :]
+        loads.extend([passes[-1], ("w2", LAST, E), ("xr",)])
+        for e in range(E):
+            raw["w2", e, e + 1] = seconds[e % 2]
         grp, codes, scales, acc, whole, relu, hid, y_sum, gated = {}, {}, {}, {}, {}, {}, {}, {}, {}
 
         def load(item):
@@ -80,20 +97,41 @@ def tile_moe_res_mlp_relu2_kernel(tc, xT, xr, w1, w2, gate, offs, out):
                 raw[item] = t
                 if s == 0:
                     nc.sync.dma_start(lists[:], offs)
+                    load(("gate",))
             elif kind == "w":
                 e, s = item[1], item[2]
-                nc.sync.dma_start(out=raw[item][:], in_=w1[e, s * K_PASS : (s + 1) * K_PASS, :].rearrange("(p j) i -> p (j i)", j=PACK))
+                if item == passes[-1]:
+                    for h in range(2):
+                        dst = raw[item][:, h * 2 * H : (h + 1) * 2 * H].rearrange("p (j i) -> p j i", j=PACK)
+                        src = w1[e, s * K_PASS :, h * H // 2 : (h + 1) * H // 2].rearrange("(p j) i -> p j i", j=PACK)
+                        nc.sync.dma_start(out=dst, in_=src)
+                    return
+                nc.sync.dma_start(out=raw[item], in_=w1[e, s * K_PASS : (s + 1) * K_PASS, :].rearrange("(p j) i -> p (j i)", j=PACK))
+            elif kind == "pair":
+                i = item[1]
+                rows = w1.rearrange("e k i -> (e k) i")[i * K_PASS : (i + 2) * K_PASS, :]
+                if i < PAIRED * PASSES:
+                    nc.sync.dma_start(out=pairs[(i + 1) // PASSES % 3][:], in_=rows.rearrange("(s p j) i -> p s (j i)", s=2, j=PACK))
+                else:
+                    load(passes[i])
             elif kind == "w2":
                 a, b = item[1:]
-                if a == 0:
-                    raw[item] = xraws.tile([P, (b - a) * PACK * N], F32, name="x_raw")
                 dst = raw[item][:, : (b - a) * PACK * N].rearrange("p (e q) -> p e q", e=b - a)
                 nc.sync.dma_start(out=dst, in_=w2[a:b].rearrange("e (p j) n -> p e (j n)", j=PACK))
             elif kind == "gate":
-                a, b = item[1:]
-                nc.sync.dma_start(out=gates[a][:], in_=gate[:, a:b])
+                nc.sync.dma_start(out=gate_rows[:E, :], in_=gate[0].rearrange("(e c) -> e c", e=E))
             else:
                 nc.sync.dma_start(out=raw[item][:, :T], in_=xr)
+
+        def spread_gate():
+            turned = psum.tile([P, P], F32, name="last0")
+            nc.tensor.transpose(turned[:], gate_rows[:], identity[:])
+            nc.scalar.activation(gate_cols[:], turned[:, :E], COPY)
+            for bank, (a, b) in enumerate(((0, TILES), (TILES, E))):
+                wide = psum.tile([P, (b - a) * C], F32, name=f"last{bank + 1}")
+                for e in range(a, b):
+                    nc.tensor.transpose(wide[:, (e - a) * C : (e - a + 1) * C], gate_cols[:, e : e + 1].to_broadcast([P, P]), identity[:])
+                nc.scalar.activation(gates[:, a * C : b * C], wide[:], COPY)
 
         def tokens(s):
             g = xgrps.tile([P, T, PACK], BF16, name="x_grp", align_bytes=64)
@@ -117,8 +155,18 @@ def tile_moe_res_mlp_relu2_kernel(tc, xT, xr, w1, w2, gate, offs, out):
             g = wgrps.tile([P, H * PACK], BF16, name="w_grp", align_bytes=64)
             grp[e, s] = g
             dst = g[:].rearrange("p (t m j) -> p m j t", t=TILES, j=PACK)
-            src = raw["w", e, s][:].rearrange("p (j m t) -> p m j t", t=TILES, j=PACK)
-            cut = (W_VECTOR_LAST if e == LAST else W_VECTOR)[s] if e else P * (s == 0)
+            if (e, s) == (LAST, PASSES - 1):
+                for h, cut in enumerate(W_VECTOR_LAST):
+                    src = raw["w", e, s][:, h * 2 * H : (h + 1) * 2 * H].rearrange("p (j m t) -> p m j t", t=TILES, j=PACK)
+                    part = dst[:, h * P // 2 : (h + 1) * P // 2]
+                    nc.vector.tensor_copy(part[:, :cut], src[:, :cut])
+                    if cut < P // 2:
+                        nc.scalar.activation(part[:, cut:], src[:, cut:], COPY)
+                return
+            src = raw["w", e, s].rearrange("p (j m t) -> p m j t", t=TILES, j=PACK)
+            cut = W_VECTOR[s] if e else P * (s == 0)
+            if (e, s) == (LAST, 1):
+                cut = W_VECTOR_LATE
             if cut:
                 nc.vector.tensor_copy(dst[:, :cut], src[:, :cut])
             if cut < P:
@@ -172,14 +220,14 @@ def tile_moe_res_mlp_relu2_kernel(tc, xT, xr, w1, w2, gate, offs, out):
                 )
 
         def step_of(e, stage):
-            return (e + 1) * PASSES + stage + (e < LAST - 1)
+            return (e + 1) * PASSES + stage
 
         def lent(e, stage):
             return raw[passes[step_of(e, stage)]]
 
         def hidden(e):
             if e < LAST:
-                r = lent(e, 0)[:].rearrange("p (j h) -> p j h", j=PACK)[:, :, :C]
+                r = lent(e, 0).rearrange("p (j h) -> p j h", j=PACK)[:, :, :C]
                 nc.scalar.activation(
                     r.rearrange("p j (c t) -> p j c t", t=TILES),
                     whole[e][:].rearrange("p t (j c) -> p j c t", j=PACK),
@@ -192,18 +240,13 @@ def tile_moe_res_mlp_relu2_kernel(tc, xT, xr, w1, w2, gate, offs, out):
 
         def square(e):
             if e < LAST:
-                if e < LAST - 1:
-                    g = lent(e, 1)[:, : C * TILES // 2].bitcast(BF16)
-                else:
-                    g = hids.tile([P, C * TILES], BF16, name="h_grp", align_bytes=64)[:]
-                nc.vector.tensor_tensor(g.rearrange("p (j q) -> p j q", j=PACK), relu[e], relu[e], MULT)
+                g = lent(e, 1)[:, : C * TILES // 2].bitcast(BF16)
+                nc.scalar.activation(g.rearrange("p (j q) -> p j q", j=PACK), relu[e], SQUARE)
             else:
                 g = hids.tile([P, C * TILES], BF16, name="h_grp", align_bytes=64)[:]
                 src = last_relu[:].rearrange("p t c -> p c t")
                 dst = g.rearrange("p (c t) -> p c t", t=TILES)
-                half = C // 2
-                nc.scalar.activation(dst[:, :half, :], src[:, :half, :], SQUARE)
-                nc.vector.tensor_tensor(dst[:, half:, :], src[:, half:, :], src[:, half:, :], MULT)
+                nc.scalar.activation(dst, src, SQUARE)
             hid[e] = g
 
         def second(e):
@@ -224,14 +267,8 @@ def tile_moe_res_mlp_relu2_kernel(tc, xT, xr, w1, w2, gate, offs, out):
             y_sum[e] = y
 
         def weigh(e):
-            first = GATE_EARLY if e * C >= GATE_EARLY else 0
-            if e in (LAST - 2, LAST):
-                gated[e] = hids.tile([P, C], F32, name="gated")[:]
-            elif e == LAST - 1:
-                gated[e] = lent(e, 2)[:, PACK * H - C :]
-            else:
-                gated[e] = lent(e, 2)[:, (PACK - 1) * H : (PACK - 1) * H + C]
-            nc.vector.tensor_tensor(gated[e], y_sum[e][:], gates[first][:, e * C - first : (e + 1) * C - first], MULT)
+            gated[e] = lent(e, 2)[:, PACK * H - C :] if e < LAST else hids.tile([P, C], F32, name="gated")[:]
+            nc.vector.tensor_tensor(gated[e], y_sum[e][:], gates[:, e * C : (e + 1) * C], MULT)
 
         def scatter(e):
             columns = C // 16
@@ -239,35 +276,37 @@ def tile_moe_res_mlp_relu2_kernel(tc, xT, xr, w1, w2, gate, offs, out):
 
         for s in range(PASSES):
             load(("x", s))
-        for item in ringed[:PASSES] + [("w2", 0, LAST - 1), ("gate", 0, GATE_EARLY)] + ringed[PASSES:AHEAD]:
+        for item in loads[:4]:
             load(item)
         for s in range(PASSES):
             tokens(s)
-        loaded = AHEAD
+            if s == 0:
+                spread_gate()
         for i in range(E * PASSES):
             e, s = divmod(i, PASSES)
-            at = ringed.index(passes[i])
-            while loaded <= min(at + AHEAD, len(ringed) - 1):
-                load(ringed[loaded])
-                if ringed[loaded] == ("w", LAST, 0):
-                    load(("gate", GATE_EARLY, S))
-                loaded = loaded + 1
-            if i == LAST * PASSES:
-                second_weights(LAST - 1, LAST, ((512, 640),))
-            due = {stage: d for d in range(LAST) for stage in range(3) if step_of(d, stage) == i}
+            if s == 2:
+                for item in loads[3 * e + 4 : 3 * e + 5]:
+                    load(item)
+            if s == 0 and e:
+                for item in loads[3 * e + 2 : 3 * e + 4]:
+                    if item[0] == "w" and e >= PAIRED:
+                        load(passes[i + PASSES])
+                    load(item)
             cast(e, s)
-            for stage, work in ((2, weigh), (2, scatter), (0, hidden), (1, square)):
-                if stage in due and not (stage == 2 and due[stage] == LAST - 1):
-                    work(due[stage])
+            if e and s == 0:
+                hidden(e - 1)
+            if e and s == 1:
+                square(e - 1)
             quantise(e, s)
-            if 1 in due:
-                second(due[1])
+            if e and s == 1:
+                second(e - 1)
             multiply(e, s)
-            if i == PASSES - 1:
-                second_weights(0, LAST - 1, ((0, 512),))
-        weigh(LAST - 1)
-        second_weights(LAST, E, ((640, 768),))
-        scatter(LAST - 1)
+            if s == PASSES - 1:
+                if e:
+                    weigh(e - 1)
+                second_weights(e, e + 1, ((e * N, (e + 1) * N),))
+                if e:
+                    scatter(e - 1)
         hidden(LAST)
         square(LAST)
         second(LAST)

@@ -30,9 +30,10 @@ W_VECTOR = (56, 64, 88)
 W_VECTOR_LAST = (52, 44)
 W_VECTOR_LATE = 88
 X_CHUNKS = ((1024, 1280), (0, 512), (512, 1024))
-OUT_PIECES = ((0, 448), (448, 832), (832, 1088), (1088, 1280))
+OUT_PIECES = ((0, 256), (256, 608), (608, 992), (992, 1280))
 LAST = E - 1
 PAIRED = 2
+W2_LOADS = {0: ("w2", 0, 2), 2: ("w2", 2, 4), 4: ("w2", 4, 5), 5: ("w2", 5, 6)}
 
 
 def tile_moe_res_mlp_relu2_kernel(tc, xT, xr, w1, w2, gate, offs, out):
@@ -71,7 +72,7 @@ def tile_moe_res_mlp_relu2_kernel(tc, xT, xr, w1, w2, gate, offs, out):
         last_relu = held.tile([P, TILES, C], F32, name="last_relu")
         pairs = [held.tile([P, 2, PACK * H], F32, name=f"pair{r}", align_bytes=64) for r in range(3)]
         singles = [held.tile([P, PACK * H], F32, name=f"single{r}", align_bytes=64) for r in range(2)]
-        seconds = [held.tile([P, PACK * N], F32, name=f"second{r}") for r in range(2)]
+        seconds = [held.tile([P, 2 * PACK * N], F32, name=f"second{r}") for r in range(2)]
 
         passes = [("w", e, s) for e in range(E) for s in range(PASSES)]
         raw = {("xr",): pairs[0][:, 1, :]}
@@ -81,14 +82,16 @@ def tile_moe_res_mlp_relu2_kernel(tc, xT, xr, w1, w2, gate, offs, out):
             i = e * PASSES + PASSES - 1
             raw[passes[i]], raw[passes[i + 1]] = pairs[(e + 1) % 3][:, 0, :], pairs[(e + 1) % 3][:, 1, :]
             raw[passes[i + 2]] = singles[e % 2][:]
-            loads.extend([("pair", i), ("w2", e, e + 1), passes[i + 2]])
+            loads.extend([("pair", i), W2_LOADS.get(e), passes[i + 2]])
         raw[passes[-1]] = pairs[0][:, 0, :]
         loads.extend([passes[-1], ("w2", LAST, E), ("xr",)])
-        for e in range(E):
-            raw["w2", e, e + 1] = seconds[e % 2]
+        for r, item in enumerate(W2_LOADS.values()):
+            raw[item] = seconds[r % 2]
         grp, codes, scales, acc, whole, relu, hid, y_sum, gated = {}, {}, {}, {}, {}, {}, {}, {}, {}
 
         def load(item):
+            if item is None:
+                return
             kind = item[0]
             if kind == "x":
                 s = item[1]
@@ -244,8 +247,8 @@ def tile_moe_res_mlp_relu2_kernel(tc, xT, xr, w1, w2, gate, offs, out):
                 nc.scalar.activation(g.rearrange("p (j q) -> p j q", j=PACK), relu[e], SQUARE)
             else:
                 g = hids.tile([P, C * TILES], BF16, name="h_grp", align_bytes=64)[:]
-                src = last_relu[:].rearrange("p t c -> p c t")
-                dst = g.rearrange("p (c t) -> p c t", t=TILES)
+                src = last_relu[:].rearrange("p t (c i) -> p c t i", i=4)
+                dst = g.rearrange("p (c i t) -> p c t i", i=4, t=TILES)
                 nc.scalar.activation(dst, src, SQUARE)
             hid[e] = g
 
@@ -289,7 +292,7 @@ def tile_moe_res_mlp_relu2_kernel(tc, xT, xr, w1, w2, gate, offs, out):
                     load(item)
             if s == 0 and e:
                 for item in loads[3 * e + 2 : 3 * e + 4]:
-                    if item[0] == "w" and e >= PAIRED:
+                    if item and item[0] == "w" and e >= PAIRED:
                         load(passes[i + PASSES])
                     load(item)
             cast(e, s)
@@ -304,7 +307,9 @@ def tile_moe_res_mlp_relu2_kernel(tc, xT, xr, w1, w2, gate, offs, out):
             if s == PASSES - 1:
                 if e:
                     weigh(e - 1)
-                second_weights(e, e + 1, ((e * N, (e + 1) * N),))
+                if e in W2_LOADS:
+                    a, b = W2_LOADS[e][1:]
+                    second_weights(a, b, ((a * N, b * N),))
                 if e:
                     scatter(e - 1)
         hidden(LAST)

@@ -24,26 +24,27 @@ PACK = 4
 K_PASS = P * PACK
 PASSES = K // K_PASS
 TILES = H // P
+LINE = 4
+LAST = E - 1
 
 X_SCALAR = 896
-W_VECTOR = (56, 64, 88)
-W_VECTOR_LAST = (52, 44)
-W_VECTOR_LATE = 88
 X_CHUNKS = ((1024, 1280), (0, 512), (512, 1024))
-OUT_PIECES = ((0, 256), (256, 608), (608, 992), (992, 1280))
-LAST = E - 1
+W_VECTOR = (56, 64, 88)
+W_VECTOR_LAST = (48, 72)
+W_VECTOR_HALVES = (44, 40)
 PAIRED = 2
 W2_LOADS = {0: ("w2", 0, 2), 2: ("w2", 2, 4), 4: ("w2", 4, 5), 5: ("w2", 5, 6)}
+OUT_PIECES = ((0, 256), (256, 608), (608, 992), (992, 1280))
 
 
 def tile_moe_res_mlp_relu2_kernel(tc, xT, xr, w1, w2, gate, offs, out):
     nc = tc.nc
     with ExitStack() as ctx:
         held = ctx.enter_context(tc.tile_pool(name="held", bufs=1))
-        xraws = ctx.enter_context(tc.tile_pool(name="xraws", bufs=3))
+        xraws = ctx.enter_context(tc.tile_pool(name="xraws", bufs=PASSES))
         xgrps = ctx.enter_context(tc.tile_pool(name="xgrps", bufs=2))
         wgrps = ctx.enter_context(tc.tile_pool(name="wgrps", bufs=3))
-        wcods = ctx.enter_context(tc.tile_pool(name="wcods", bufs=6))
+        wcods = ctx.enter_context(tc.tile_pool(name="wcods", bufs=2 * PASSES))
         hids = ctx.enter_context(tc.tile_pool(name="hids", bufs=2))
         psum = ctx.enter_context(tc.psum_pool(name="psum", bufs=1))
         ypsum = ctx.enter_context(tc.psum_pool(name="ypsum", bufs=2))
@@ -74,57 +75,51 @@ def tile_moe_res_mlp_relu2_kernel(tc, xT, xr, w1, w2, gate, offs, out):
         singles = [held.tile([P, PACK * H], F32, name=f"single{r}", align_bytes=64) for r in range(2)]
         seconds = [held.tile([P, 2 * PACK * N], F32, name=f"second{r}") for r in range(2)]
 
-        passes = [("w", e, s) for e in range(E) for s in range(PASSES)]
-        raw = {("xr",): pairs[0][:, 1, :]}
-        loads = [("pair", 0)]
-        raw[passes[0]], raw[passes[1]] = pairs[0][:, 0, :], pairs[0][:, 1, :]
+        raw = {(0, 0): pairs[0][:, 0, :], (0, 1): pairs[0][:, 1, :]}
         for e in range(LAST):
-            i = e * PASSES + PASSES - 1
-            raw[passes[i]], raw[passes[i + 1]] = pairs[(e + 1) % 3][:, 0, :], pairs[(e + 1) % 3][:, 1, :]
-            raw[passes[i + 2]] = singles[e % 2][:]
-            loads.extend([("pair", i), W2_LOADS.get(e), passes[i + 2]])
-        raw[passes[-1]] = pairs[0][:, 0, :]
-        loads.extend([passes[-1], ("w2", LAST, E), ("xr",)])
-        for r, item in enumerate(W2_LOADS.values()):
-            raw[item] = seconds[r % 2]
-        grp, codes, scales, acc, whole, relu, hid, y_sum, gated = {}, {}, {}, {}, {}, {}, {}, {}, {}
+            raw[e, 2], raw[e + 1, 0] = (pairs[(e + 1) % len(pairs)][:, half, :] for half in range(2))
+            raw[e + 1, 1] = singles[e % len(singles)][:]
+        raw[LAST, 2] = pairs[0][:, 0, :]
+        xr_raw = pairs[0][:, 1, :T]
+        w2_raw = {item: seconds[r % len(seconds)] for r, item in enumerate(W2_LOADS.values())}
+        x_raw, grp, codes, scales, acc, whole, relu, hid, y_sum, gated = {}, {}, {}, {}, {}, {}, {}, {}, {}, {}
 
-        def load(item):
-            if item is None:
+        def load_tokens(s):
+            t = xraws.tile([P, PACK, T], F32, name="x_raw")
+            nc.sync.dma_start(out=t[:], in_=xT[s * K_PASS : (s + 1) * K_PASS, :].rearrange("(p j) t -> p j t", j=PACK))
+            x_raw[s] = t
+
+        def load_pass(e, s):
+            rows = w1[e, s * K_PASS : (s + 1) * K_PASS, :]
+            if (e, s) != (LAST, PASSES - 1):
+                nc.sync.dma_start(out=raw[e, s], in_=rows.rearrange("(p j) i -> p (j i)", j=PACK))
                 return
-            kind = item[0]
-            if kind == "x":
-                s = item[1]
-                t = xraws.tile([P, PACK, T], F32, name="x_raw")
-                nc.sync.dma_start(out=t[:], in_=xT[s * K_PASS : (s + 1) * K_PASS, :].rearrange("(p j) t -> p j t", j=PACK))
-                raw[item] = t
-                if s == 0:
-                    nc.sync.dma_start(lists[:], offs)
-                    load(("gate",))
-            elif kind == "w":
-                e, s = item[1], item[2]
-                if item == passes[-1]:
-                    for h in range(2):
-                        dst = raw[item][:, h * 2 * H : (h + 1) * 2 * H].rearrange("p (j i) -> p j i", j=PACK)
-                        src = w1[e, s * K_PASS :, h * H // 2 : (h + 1) * H // 2].rearrange("(p j) i -> p j i", j=PACK)
-                        nc.sync.dma_start(out=dst, in_=src)
-                    return
-                nc.sync.dma_start(out=raw[item], in_=w1[e, s * K_PASS : (s + 1) * K_PASS, :].rearrange("(p j) i -> p (j i)", j=PACK))
-            elif kind == "pair":
-                i = item[1]
-                rows = w1.rearrange("e k i -> (e k) i")[i * K_PASS : (i + 2) * K_PASS, :]
-                if i < PAIRED * PASSES:
-                    nc.sync.dma_start(out=pairs[(i + 1) // PASSES % 3][:], in_=rows.rearrange("(s p j) i -> p s (j i)", s=2, j=PACK))
-                else:
-                    load(passes[i])
-            elif kind == "w2":
-                a, b = item[1:]
-                dst = raw[item][:, : (b - a) * PACK * N].rearrange("p (e q) -> p e q", e=b - a)
-                nc.sync.dma_start(out=dst, in_=w2[a:b].rearrange("e (p j) n -> p e (j n)", j=PACK))
-            elif kind == "gate":
-                nc.sync.dma_start(out=gate_rows[:E, :], in_=gate[0].rearrange("(e c) -> e c", e=E))
+            for half in range(2):
+                dst = raw[e, s][:, half * 2 * H : (half + 1) * 2 * H].rearrange("p (j i) -> p j i", j=PACK)
+                src = rows[:, half * H // 2 : (half + 1) * H // 2].rearrange("(p j) i -> p j i", j=PACK)
+                nc.sync.dma_start(out=dst, in_=src)
+
+        def load_pair(first, pair):
+            rows = w1.rearrange("e k i -> (e k) i")[first * K_PASS : (first + 2) * K_PASS, :]
+            nc.sync.dma_start(out=pair[:], in_=rows.rearrange("(s p j) i -> p s (j i)", s=2, j=PACK))
+
+        def load_third(e):
+            if e < PAIRED:
+                load_pair(e * PASSES + PASSES - 1, pairs[(e + 1) % len(pairs)])
             else:
-                nc.sync.dma_start(out=raw[item][:, :T], in_=xr)
+                load_pass(e, PASSES - 1)
+
+        def load_behind_third(e):
+            if e in W2_LOADS:
+                a, b = W2_LOADS[e][1:]
+                dst = w2_raw[W2_LOADS[e]][:, : (b - a) * PACK * N].rearrange("p (e q) -> p e q", e=b - a)
+                nc.sync.dma_start(out=dst, in_=w2[a:b].rearrange("e (p j) n -> p e (j n)", j=PACK))
+            if e == LAST:
+                nc.sync.dma_start(out=xr_raw, in_=xr)
+                return
+            if e >= PAIRED:
+                load_pass(e + 1, 0)
+            load_pass(e + 1, 1)
 
         def spread_gate():
             turned = psum.tile([P, P], F32, name="last0")
@@ -133,17 +128,19 @@ def tile_moe_res_mlp_relu2_kernel(tc, xT, xr, w1, w2, gate, offs, out):
             for bank, (a, b) in enumerate(((0, TILES), (TILES, E))):
                 wide = psum.tile([P, (b - a) * C], F32, name=f"last{bank + 1}")
                 for e in range(a, b):
-                    nc.tensor.transpose(wide[:, (e - a) * C : (e - a + 1) * C], gate_cols[:, e : e + 1].to_broadcast([P, P]), identity[:])
+                    column = gate_cols[:, e : e + 1].to_broadcast([P, P])
+                    nc.tensor.transpose(wide[:, (e - a) * C : (e - a + 1) * C], column, identity[:])
                 nc.scalar.activation(gates[:, a * C : b * C], wide[:], COPY)
 
         def tokens(s):
             g = xgrps.tile([P, T, PACK], BF16, name="x_grp", align_bytes=64)
-            dst = g[:].rearrange("p (c i) t -> p c t i", i=4)
-            src = raw["x", s][:].rearrange("p t (c i) -> p c t i", i=4)
-            for a, b in ((0, 512), (512, X_SCALAR)):
-                nc.scalar.activation(dst[:, a // 4 : b // 4], src[:, a // 4 : b // 4], COPY)
-            nc.vector.tensor_copy(dst[:, X_SCALAR // 4 :], src[:, X_SCALAR // 4 :])
-            flat = g[:].rearrange("p n t -> p (n t)")
+            dst = g[:].rearrange("p (c i) j -> p c j i", i=LINE)
+            src = x_raw[s][:].rearrange("p j (c i) -> p c j i", i=LINE)
+            first_chunk = X_CHUNKS[1][1]
+            for a, b in ((0, first_chunk), (first_chunk, X_SCALAR)):
+                nc.scalar.activation(dst[:, a // LINE : b // LINE], src[:, a // LINE : b // LINE], COPY)
+            nc.vector.tensor_copy(dst[:, X_SCALAR // LINE :], src[:, X_SCALAR // LINE :])
+            flat = g[:].rearrange("p n j -> p (n j)")
             for a, b in X_CHUNKS:
                 nc.vector.quantize_mx(
                     out=words[s][:, a:b].bitcast(FP8X4),
@@ -154,26 +151,26 @@ def tile_moe_res_mlp_relu2_kernel(tc, xT, xr, w1, w2, gate, offs, out):
             if s == PASSES - 1:
                 nc.vector.tensor_copy(slot_planes[:], planes[:].indirect(lists[:]))
 
-        def cast(e, s):
-            g = wgrps.tile([P, H * PACK], BF16, name="w_grp", align_bytes=64)
-            grp[e, s] = g
-            dst = g[:].rearrange("p (t m j) -> p m j t", t=TILES, j=PACK)
-            if (e, s) == (LAST, PASSES - 1):
-                for h, cut in enumerate(W_VECTOR_LAST):
-                    src = raw["w", e, s][:, h * 2 * H : (h + 1) * 2 * H].rearrange("p (j m t) -> p m j t", t=TILES, j=PACK)
-                    part = dst[:, h * P // 2 : (h + 1) * P // 2]
-                    nc.vector.tensor_copy(part[:, :cut], src[:, :cut])
-                    if cut < P // 2:
-                        nc.scalar.activation(part[:, cut:], src[:, cut:], COPY)
-                return
-            src = raw["w", e, s].rearrange("p (j m t) -> p m j t", t=TILES, j=PACK)
-            cut = W_VECTOR[s] if e else P * (s == 0)
-            if (e, s) == (LAST, 1):
-                cut = W_VECTOR_LATE
+        def round_groups(dst, src, cut):
             if cut:
                 nc.vector.tensor_copy(dst[:, :cut], src[:, :cut])
             if cut < P:
                 nc.scalar.activation(dst[:, cut:], src[:, cut:], COPY)
+
+        def round_pass(e, s):
+            g = wgrps.tile([P, H * PACK], BF16, name="w_grp", align_bytes=64)
+            grp[e, s] = g
+            dst = g[:].rearrange("p (t m j) -> p m j t", t=TILES, j=PACK)
+            if (e, s) == (LAST, PASSES - 1):
+                for half, cut in enumerate(W_VECTOR_HALVES):
+                    src = raw[e, s][:, half * 2 * H : (half + 1) * 2 * H].rearrange("p (j m t) -> p m j t", t=TILES, j=PACK)
+                    round_groups(dst[:, half * P // 2 : (half + 1) * P // 2], src, cut)
+                return
+            if e == 0:
+                cut = P if s == 0 else 0
+            else:
+                cut = (W_VECTOR_LAST if e == LAST else W_VECTOR)[s]
+            round_groups(dst, raw[e, s].rearrange("p (j m t) -> p m j t", t=TILES, j=PACK), cut)
 
         def quantise(e, s):
             c = wcods.tile([P, H], U32, name="w_codes", align_bytes=64)
@@ -184,17 +181,17 @@ def tile_moe_res_mlp_relu2_kernel(tc, xT, xr, w1, w2, gate, offs, out):
                 nc.vector.quantize_mx(out=c[:, a:b].bitcast(FP8X4), scales=z[:, a:b], in_=grp[e, s][:, PACK * a : PACK * b])
             codes[e, s], scales[e, s] = c, z
 
-        def second_weights(a, b, chunks):
+        def second_weights(item):
+            a, b = item[1:]
             for e in range(a, b):
-                dst = w2_grp[:, e * N * PACK : (e + 1) * N * PACK].rearrange("p (c i j) -> p c j i", i=4, j=PACK)
-                src = raw["w2", a, b][:, (e - a) * N * PACK : (e - a + 1) * N * PACK].rearrange("p (j c i) -> p c j i", i=4, j=PACK)
-                nc.scalar.activation(dst, src, COPY)
-            for lo, hi in chunks:
-                nc.vector.quantize_mx(
-                    out=w2_codes[:, lo:hi].bitcast(FP8X4),
-                    scales=w2_scales[:, lo:hi],
-                    in_=w2_grp[:, PACK * lo : PACK * hi],
-                )
+                dst = w2_grp[:, e * N * PACK : (e + 1) * N * PACK].rearrange("p (c i j) -> p c j i", i=LINE, j=PACK)
+                src = w2_raw[item][:, (e - a) * N * PACK : (e - a + 1) * N * PACK]
+                nc.scalar.activation(dst, src.rearrange("p (j c i) -> p c j i", i=LINE, j=PACK), COPY)
+            nc.vector.quantize_mx(
+                out=w2_codes[:, a * N : b * N].bitcast(FP8X4),
+                scales=w2_scales[:, a * N : b * N],
+                in_=w2_grp[:, PACK * a * N : PACK * b * N],
+            )
 
         def multiply(e, s):
             if e < LAST:
@@ -222,15 +219,9 @@ def tile_moe_res_mlp_relu2_kernel(tc, xT, xr, w1, w2, gate, offs, out):
                     stop=(k == PASSES - 1),
                 )
 
-        def step_of(e, stage):
-            return (e + 1) * PASSES + stage
-
-        def lent(e, stage):
-            return raw[passes[step_of(e, stage)]]
-
-        def hidden(e):
+        def rectify(e):
             if e < LAST:
-                r = lent(e, 0).rearrange("p (j h) -> p j h", j=PACK)[:, :, :C]
+                r = raw[e + 1, 0].rearrange("p (j h) -> p j h", j=PACK)[:, :, :C]
                 nc.scalar.activation(
                     r.rearrange("p j (c t) -> p j c t", t=TILES),
                     whole[e][:].rearrange("p t (j c) -> p j c t", j=PACK),
@@ -243,16 +234,16 @@ def tile_moe_res_mlp_relu2_kernel(tc, xT, xr, w1, w2, gate, offs, out):
 
         def square(e):
             if e < LAST:
-                g = lent(e, 1)[:, : C * TILES // 2].bitcast(BF16)
+                g = raw[e + 1, 1][:, : C * TILES // 2].bitcast(BF16)
                 nc.scalar.activation(g.rearrange("p (j q) -> p j q", j=PACK), relu[e], SQUARE)
             else:
                 g = hids.tile([P, C * TILES], BF16, name="h_grp", align_bytes=64)[:]
-                src = last_relu[:].rearrange("p t (c i) -> p c t i", i=4)
-                dst = g.rearrange("p (c i t) -> p c t i", i=4, t=TILES)
+                src = last_relu[:].rearrange("p t (c i) -> p c t i", i=LINE)
+                dst = g.rearrange("p (c i t) -> p c t i", i=LINE, t=TILES)
                 nc.scalar.activation(dst, src, SQUARE)
             hid[e] = g
 
-        def second(e):
+        def second_product(e):
             c = hids.tile([P, C], U32, name="h_codes", align_bytes=64)
             z = hids.tile([P, C], U8, name="h_scales", align_bytes=64)
             nc.vector.quantize_mx(out=c[:].bitcast(FP8X4), scales=z[:], in_=hid[e])
@@ -270,54 +261,61 @@ def tile_moe_res_mlp_relu2_kernel(tc, xT, xr, w1, w2, gate, offs, out):
             y_sum[e] = y
 
         def weigh(e):
-            gated[e] = lent(e, 2)[:, PACK * H - C :] if e < LAST else hids.tile([P, C], F32, name="gated")[:]
+            gated[e] = raw[e + 1, 2][:, PACK * H - C :] if e < LAST else hids.tile([P, C], F32, name="gated")[:]
             nc.vector.tensor_tensor(gated[e], y_sum[e][:], gates[:, e * C : (e + 1) * C], MULT)
 
         def scatter(e):
             columns = C // 16
-            nc.vector.tensor_tensor(window[:].indirect(lists[:, e * columns : (e + 1) * columns]), gated[e], zeros[:], ADD)
+            offsets = lists[:, e * columns : (e + 1) * columns]
+            nc.vector.tensor_tensor(window[:].indirect(offsets), gated[e], zeros[:], ADD)
 
-        for s in range(PASSES):
-            load(("x", s))
-        for item in loads[:4]:
-            load(item)
+        load_tokens(0)
+        nc.sync.dma_start(lists[:], offs)
+        nc.sync.dma_start(out=gate_rows[:E, :], in_=gate[0].rearrange("(e c) -> e c", e=E))
+        for s in range(1, PASSES):
+            load_tokens(s)
+        load_pair(0, pairs[0])
+        load_third(0)
+        load_behind_third(0)
         for s in range(PASSES):
             tokens(s)
             if s == 0:
                 spread_gate()
-        for i in range(E * PASSES):
-            e, s = divmod(i, PASSES)
-            if s == 2:
-                for item in loads[3 * e + 4 : 3 * e + 5]:
-                    load(item)
-            if s == 0 and e:
-                for item in loads[3 * e + 2 : 3 * e + 4]:
-                    if item and item[0] == "w" and e >= PAIRED:
-                        load(passes[i + PASSES])
-                    load(item)
-            cast(e, s)
-            if e and s == 0:
-                hidden(e - 1)
-            if e and s == 1:
+
+        for e in range(E):
+            if e:
+                load_behind_third(e)
+            round_pass(e, 0)
+            if e:
+                rectify(e - 1)
+            quantise(e, 0)
+            multiply(e, 0)
+
+            round_pass(e, 1)
+            if e:
                 square(e - 1)
-            quantise(e, s)
-            if e and s == 1:
-                second(e - 1)
-            multiply(e, s)
-            if s == PASSES - 1:
-                if e:
-                    weigh(e - 1)
-                if e in W2_LOADS:
-                    a, b = W2_LOADS[e][1:]
-                    second_weights(a, b, ((a * N, b * N),))
-                if e:
-                    scatter(e - 1)
-        hidden(LAST)
+            quantise(e, 1)
+            if e:
+                second_product(e - 1)
+            multiply(e, 1)
+
+            if e < LAST:
+                load_third(e + 1)
+            round_pass(e, 2)
+            quantise(e, 2)
+            multiply(e, 2)
+            if e:
+                weigh(e - 1)
+            if e in W2_LOADS:
+                second_weights(W2_LOADS[e])
+            if e:
+                scatter(e - 1)
+        rectify(LAST)
         square(LAST)
-        second(LAST)
+        second_product(LAST)
         weigh(LAST)
         scatter(LAST)
 
         for a, b in OUT_PIECES:
-            nc.vector.tensor_tensor(result[:, a:b], window[:, a:b], raw["xr",][:, a:b], ADD)
+            nc.vector.tensor_tensor(result[:, a:b], window[:, a:b], xr_raw[:, a:b], ADD)
             nc.sync.dma_start(out=out[:, a:b], in_=result[:, a:b])

@@ -33,7 +33,8 @@ W_VECTOR = (56, 64, 88)
 W_VECTOR_LAST = (48, 72)
 W_VECTOR_HALVES = (44, 40)
 PAIRED = 2
-W2_LOADS = {0: ("w2", 0, 2), 2: ("w2", 2, 4), 4: ("w2", 4, 5), 5: ("w2", 5, 6)}
+W2_LOADS = {0: ("w2", 0, 2), 2: ("w2", 2, 4)}
+W2_LATE = (("w2", 4, 5), ("w2", 5, 6))
 OUT_PIECES = ((0, 256), (256, 608), (608, 992), (992, 1280))
 
 
@@ -70,10 +71,9 @@ def tile_moe_res_mlp_relu2_kernel(tc, xT, xr, w1, w2, gate, offs, out):
         identity = held.tile([P, P], F32, name="identity")
         make_identity(nc, identity[:])
         result = held.tile([P, T], F32, name="result")
-        last_relu = held.tile([P, TILES, C], F32, name="last_relu")
         pairs = [held.tile([P, 2, PACK * H], F32, name=f"pair{r}", align_bytes=64) for r in range(3)]
         singles = [held.tile([P, PACK * H], F32, name=f"single{r}", align_bytes=64) for r in range(2)]
-        seconds = [held.tile([P, 2 * PACK * N], F32, name=f"second{r}") for r in range(2)]
+        seconds = [held.tile([P, 2 * PACK * N], F32, name=f"second{r}", align_bytes=64) for r in range(2)]
 
         raw = {(0, 0): pairs[0][:, 0, :], (0, 1): pairs[0][:, 1, :]}
         for e in range(LAST):
@@ -81,8 +81,10 @@ def tile_moe_res_mlp_relu2_kernel(tc, xT, xr, w1, w2, gate, offs, out):
             raw[e + 1, 1] = singles[e % len(singles)][:]
         raw[LAST, 2] = pairs[0][:, 0, :]
         xr_raw = pairs[0][:, 1, :T]
-        w2_raw = {item: seconds[r % len(seconds)] for r, item in enumerate(W2_LOADS.values())}
+        w2_raw = {item: seconds[r % len(seconds)] for r, item in enumerate(list(W2_LOADS.values()) + list(W2_LATE))}
+        last_relu = w2_raw[W2_LATE[0]][:, : TILES * C].rearrange("p (t c) -> p t c", t=TILES)
         x_raw, grp, codes, scales, acc, whole, relu, hid, y_sum, gated = {}, {}, {}, {}, {}, {}, {}, {}, {}, {}
+        h_mx = {}
 
         def load_tokens(s):
             t = xraws.tile([P, PACK, T], F32, name="x_raw")
@@ -109,12 +111,17 @@ def tile_moe_res_mlp_relu2_kernel(tc, xT, xr, w1, w2, gate, offs, out):
             else:
                 load_pass(e, PASSES - 1)
 
+        def load_second(item):
+            a, b = item[1:]
+            dst = w2_raw[item][:, : (b - a) * PACK * N].rearrange("p (e q) -> p e q", e=b - a)
+            nc.sync.dma_start(out=dst, in_=w2[a:b].rearrange("e (p j) n -> p e (j n)", j=PACK))
+
         def load_behind_third(e):
             if e in W2_LOADS:
-                a, b = W2_LOADS[e][1:]
-                dst = w2_raw[W2_LOADS[e]][:, : (b - a) * PACK * N].rearrange("p (e q) -> p e q", e=b - a)
-                nc.sync.dma_start(out=dst, in_=w2[a:b].rearrange("e (p j) n -> p e (j n)", j=PACK))
+                load_second(W2_LOADS[e])
             if e == LAST:
+                for item in W2_LATE:
+                    load_second(item)
                 nc.sync.dma_start(out=xr_raw, in_=xr)
                 return
             if e >= PAIRED:
@@ -162,9 +169,16 @@ def tile_moe_res_mlp_relu2_kernel(tc, xT, xr, w1, w2, gate, offs, out):
             grp[e, s] = g
             dst = g[:].rearrange("p (t m j) -> p m j t", t=TILES, j=PACK)
             if (e, s) == (LAST, PASSES - 1):
+                c = wcods.tile([P, H], U32, name="w_codes", align_bytes=64)
+                z = wcods.tile([P, H], U8, name="w_scales", align_bytes=64)
+                codes[e, s], scales[e, s] = c, z
                 for half, cut in enumerate(W_VECTOR_HALVES):
                     src = raw[e, s][:, half * 2 * H : (half + 1) * 2 * H].rearrange("p (j m t) -> p m j t", t=TILES, j=PACK)
                     round_groups(dst[:, half * P // 2 : (half + 1) * P // 2], src, cut)
+                    for t in range(TILES):
+                        a = t * P + half * P // 2
+                        b = a + P // 2
+                        nc.vector.quantize_mx(out=c[:, a:b].bitcast(FP8X4), scales=z[:, a:b], in_=g[:, PACK * a : PACK * b])
                 return
             if e == 0:
                 cut = P if s == 0 else 0
@@ -173,20 +187,26 @@ def tile_moe_res_mlp_relu2_kernel(tc, xT, xr, w1, w2, gate, offs, out):
             round_groups(dst, raw[e, s].rearrange("p (j m t) -> p m j t", t=TILES, j=PACK), cut)
 
         def quantise(e, s):
+            if (e, s) == (LAST, PASSES - 1):
+                return
             c = wcods.tile([P, H], U32, name="w_codes", align_bytes=64)
             z = wcods.tile([P, H], U8, name="w_scales", align_bytes=64)
-            width = P if (e, s) == (LAST, PASSES - 1) else H
-            for a in range(0, H, width):
-                b = a + width
-                nc.vector.quantize_mx(out=c[:, a:b].bitcast(FP8X4), scales=z[:, a:b], in_=grp[e, s][:, PACK * a : PACK * b])
+            nc.vector.quantize_mx(out=c[:].bitcast(FP8X4), scales=z[:], in_=grp[e, s][:])
             codes[e, s], scales[e, s] = c, z
 
-        def second_weights(item):
+        def round_second(item):
             a, b = item[1:]
             for e in range(a, b):
                 dst = w2_grp[:, e * N * PACK : (e + 1) * N * PACK].rearrange("p (c i j) -> p c j i", i=LINE, j=PACK)
                 src = w2_raw[item][:, (e - a) * N * PACK : (e - a + 1) * N * PACK]
-                nc.scalar.activation(dst, src.rearrange("p (j c i) -> p c j i", i=LINE, j=PACK), COPY)
+                src = src.rearrange("p (j c i) -> p c j i", i=LINE, j=PACK)
+                if e == LAST:
+                    nc.vector.tensor_copy(dst, src)
+                else:
+                    nc.scalar.activation(dst, src, COPY)
+
+        def quantise_second(item):
+            a, b = item[1:]
             nc.vector.quantize_mx(
                 out=w2_codes[:, a * N : b * N].bitcast(FP8X4),
                 scales=w2_scales[:, a * N : b * N],
@@ -237,16 +257,20 @@ def tile_moe_res_mlp_relu2_kernel(tc, xT, xr, w1, w2, gate, offs, out):
                 g = raw[e + 1, 1][:, : C * TILES // 2].bitcast(BF16)
                 nc.scalar.activation(g.rearrange("p (j q) -> p j q", j=PACK), relu[e], SQUARE)
             else:
-                g = hids.tile([P, C * TILES], BF16, name="h_grp", align_bytes=64)[:]
-                src = last_relu[:].rearrange("p t (c i) -> p c t i", i=LINE)
+                g = w2_raw[W2_LATE[1]][:, : C * TILES // 2].bitcast(BF16)
+                src = last_relu.rearrange("p t (c i) -> p c t i", i=LINE)
                 dst = g.rearrange("p (c i t) -> p c t i", i=LINE, t=TILES)
                 nc.scalar.activation(dst, src, SQUARE)
             hid[e] = g
 
-        def second_product(e):
+        def quantise_hidden(e):
             c = hids.tile([P, C], U32, name="h_codes", align_bytes=64)
             z = hids.tile([P, C], U8, name="h_scales", align_bytes=64)
             nc.vector.quantize_mx(out=c[:].bitcast(FP8X4), scales=z[:], in_=hid[e])
+            h_mx[e] = c, z
+
+        def second_product(e):
+            c, z = h_mx[e]
             y = ypsum.tile([P, C], F32, name="y")
             cols = slice(e * N, (e + 1) * N)
             nc.tensor.matmul_mx(
@@ -261,13 +285,17 @@ def tile_moe_res_mlp_relu2_kernel(tc, xT, xr, w1, w2, gate, offs, out):
             y_sum[e] = y
 
         def weigh(e):
-            gated[e] = raw[e + 1, 2][:, PACK * H - C :] if e < LAST else hids.tile([P, C], F32, name="gated")[:]
+            if e < LAST - 1:
+                gated[e] = raw[e + 1, 2][:, PACK * H - C :]
+            elif e < LAST:
+                gated[e] = w2_raw[W2_LATE[1]][:, PACK * N - C : PACK * N]
+            else:
+                gated[e] = hids.tile([P, C], F32, name="gated")[:]
             nc.vector.tensor_tensor(gated[e], y_sum[e][:], gates[:, e * C : (e + 1) * C], MULT)
 
-        def scatter(e):
-            columns = C // 16
-            offsets = lists[:, e * columns : (e + 1) * columns]
-            nc.vector.tensor_tensor(window[:].indirect(offsets), gated[e], zeros[:], ADD)
+        def scatter(e, a=0, b=C, second=None):
+            offsets = lists[:, (e * C + a) // 16 : (e * C + b) // 16]
+            nc.vector.tensor_tensor(window[:].indirect(offsets), gated[e][:, a:b], zeros[:, a:b] if second is None else second, ADD)
 
         load_tokens(0)
         nc.sync.dma_start(lists[:], offs)
@@ -296,6 +324,8 @@ def tile_moe_res_mlp_relu2_kernel(tc, xT, xr, w1, w2, gate, offs, out):
                 square(e - 1)
             quantise(e, 1)
             if e:
+                quantise_hidden(e - 1)
+            if 0 < e < LAST:
                 second_product(e - 1)
             multiply(e, 1)
 
@@ -304,15 +334,27 @@ def tile_moe_res_mlp_relu2_kernel(tc, xT, xr, w1, w2, gate, offs, out):
             round_pass(e, 2)
             quantise(e, 2)
             multiply(e, 2)
-            if e:
+            if 0 < e < LAST:
                 weigh(e - 1)
             if e in W2_LOADS:
-                second_weights(W2_LOADS[e])
-            if e:
+                round_second(W2_LOADS[e])
+                quantise_second(W2_LOADS[e])
+            if 0 < e < LAST:
                 scatter(e - 1)
+        round_second(W2_LATE[0])
+        quantise_second(W2_LATE[0])
+        second_product(LAST - 1)
         rectify(LAST)
+        round_second(W2_LATE[1])
+        weigh(LAST - 1)
+        quantise_second(W2_LATE[1])
+        scatter(LAST - 1, 0, C // 2)
         square(LAST)
+        late_zeros = last_relu[:, 0, : C // 2]
+        nc.scalar.activation(late_zeros, zeros[:, : C // 2], COPY)
+        quantise_hidden(LAST)
         second_product(LAST)
+        scatter(LAST - 1, C // 2, C, late_zeros)
         weigh(LAST)
         scatter(LAST)
 

@@ -34,7 +34,7 @@ W_VECTOR_LAST = (48, 72)
 W_VECTOR_HALVES = (44, 40)
 PAIRED = 2
 W2_LOADS = {0: ("w2", 0, 2), 2: ("w2", 2, 4)}
-W2_LATE = (("w2", 4, 5), ("w2", 5, 6))
+W2_LATE = ("w2", 4, 6)
 OUT_PIECES = ((0, 256), (256, 608), (608, 992), (992, 1280))
 
 
@@ -81,8 +81,8 @@ def tile_moe_res_mlp_relu2_kernel(tc, xT, xr, w1, w2, gate, offs, out):
             raw[e + 1, 1] = singles[e % len(singles)][:]
         raw[LAST, 2] = pairs[0][:, 0, :]
         xr_raw = pairs[0][:, 1, :T]
-        w2_raw = {item: seconds[r % len(seconds)] for r, item in enumerate(list(W2_LOADS.values()) + list(W2_LATE))}
-        last_relu = w2_raw[W2_LATE[0]][:, : TILES * C].rearrange("p (t c) -> p t c", t=TILES)
+        w2_raw = {item: seconds[r % len(seconds)] for r, item in enumerate(list(W2_LOADS.values()) + [W2_LATE])}
+        last_relu = seconds[1][:, : TILES * C].rearrange("p (t c) -> p t c", t=TILES)
         x_raw, grp, codes, scales, acc, whole, relu, hid, y_sum, gated = {}, {}, {}, {}, {}, {}, {}, {}, {}, {}
         h_mx = {}
 
@@ -120,8 +120,7 @@ def tile_moe_res_mlp_relu2_kernel(tc, xT, xr, w1, w2, gate, offs, out):
             if e in W2_LOADS:
                 load_second(W2_LOADS[e])
             if e == LAST:
-                for item in W2_LATE:
-                    load_second(item)
+                load_second(W2_LATE)
                 nc.sync.dma_start(out=xr_raw, in_=xr)
                 return
             if e >= PAIRED:
@@ -200,13 +199,12 @@ def tile_moe_res_mlp_relu2_kernel(tc, xT, xr, w1, w2, gate, offs, out):
                 dst = w2_grp[:, e * N * PACK : (e + 1) * N * PACK].rearrange("p (c i j) -> p c j i", i=LINE, j=PACK)
                 src = w2_raw[item][:, (e - a) * N * PACK : (e - a + 1) * N * PACK]
                 src = src.rearrange("p (j c i) -> p c j i", i=LINE, j=PACK)
-                if e == LAST:
+                if item == W2_LATE:
                     nc.vector.tensor_copy(dst, src)
                 else:
                     nc.scalar.activation(dst, src, COPY)
 
-        def quantise_second(item):
-            a, b = item[1:]
+        def quantise_second(a, b):
             nc.vector.quantize_mx(
                 out=w2_codes[:, a * N : b * N].bitcast(FP8X4),
                 scales=w2_scales[:, a * N : b * N],
@@ -257,7 +255,7 @@ def tile_moe_res_mlp_relu2_kernel(tc, xT, xr, w1, w2, gate, offs, out):
                 g = raw[e + 1, 1][:, : C * TILES // 2].bitcast(BF16)
                 nc.scalar.activation(g.rearrange("p (j q) -> p j q", j=PACK), relu[e], SQUARE)
             else:
-                g = w2_raw[W2_LATE[1]][:, : C * TILES // 2].bitcast(BF16)
+                g = w2_raw[W2_LATE][:, : C * TILES // 2].bitcast(BF16)
                 src = last_relu.rearrange("p t (c i) -> p c t i", i=LINE)
                 dst = g.rearrange("p (c i t) -> p c t i", i=LINE, t=TILES)
                 nc.scalar.activation(dst, src, SQUARE)
@@ -287,8 +285,6 @@ def tile_moe_res_mlp_relu2_kernel(tc, xT, xr, w1, w2, gate, offs, out):
         def weigh(e):
             if e < LAST - 1:
                 gated[e] = raw[e + 1, 2][:, PACK * H - C :]
-            elif e < LAST:
-                gated[e] = w2_raw[W2_LATE[1]][:, PACK * N - C : PACK * N]
             else:
                 gated[e] = hids.tile([P, C], F32, name="gated")[:]
             nc.vector.tensor_tensor(gated[e], y_sum[e][:], gates[:, e * C : (e + 1) * C], MULT)
@@ -338,23 +334,19 @@ def tile_moe_res_mlp_relu2_kernel(tc, xT, xr, w1, w2, gate, offs, out):
                 weigh(e - 1)
             if e in W2_LOADS:
                 round_second(W2_LOADS[e])
-                quantise_second(W2_LOADS[e])
+                quantise_second(*W2_LOADS[e][1:])
             if 0 < e < LAST:
                 scatter(e - 1)
-        round_second(W2_LATE[0])
-        quantise_second(W2_LATE[0])
+        round_second(W2_LATE)
+        quantise_second(LAST - 1, LAST)
         second_product(LAST - 1)
+        quantise_second(LAST, E)
         rectify(LAST)
-        round_second(W2_LATE[1])
         weigh(LAST - 1)
-        quantise_second(W2_LATE[1])
-        scatter(LAST - 1, 0, C // 2)
         square(LAST)
-        late_zeros = last_relu[:, 0, : C // 2]
-        nc.scalar.activation(late_zeros, zeros[:, : C // 2], COPY)
         quantise_hidden(LAST)
         second_product(LAST)
-        scatter(LAST - 1, C // 2, C, late_zeros)
+        scatter(LAST - 1)
         weigh(LAST)
         scatter(LAST)
 

@@ -30,8 +30,9 @@ LAST = E - 1
 X_SCALAR = 896
 X_CHUNKS = ((1024, 1280), (0, 512), (512, 1024))
 W_VECTOR = (56, 64, 88)
-W_VECTOR_LAST = (48, 72)
-W_VECTOR_HALVES = (44, 40)
+W_VECTOR_LAST = (56, 72)
+LAST_SPLIT = 48
+LAST_VECTOR = (32, 104)
 PAIRED = 2
 W2_LOADS = {0: ("w2", 0, 2), 2: ("w2", 2, 4)}
 W2_LATE = ("w2", 4, 6)
@@ -96,9 +97,9 @@ def tile_moe_res_mlp_relu2_kernel(tc, xT, xr, w1, w2, gate, offs, out):
             if (e, s) != (LAST, PASSES - 1):
                 nc.sync.dma_start(out=raw[e, s], in_=rows.rearrange("(p j) i -> p (j i)", j=PACK))
                 return
-            for half in range(2):
-                dst = raw[e, s][:, half * 2 * H : (half + 1) * 2 * H].rearrange("p (j i) -> p j i", j=PACK)
-                src = rows[:, half * H // 2 : (half + 1) * H // 2].rearrange("(p j) i -> p j i", j=PACK)
+            for a, b in ((0, LAST_SPLIT), (LAST_SPLIT, P)):
+                dst = raw[e, s][:, a * PACK * TILES : b * PACK * TILES].rearrange("p (j i) -> p j i", j=PACK)
+                src = rows[:, a * TILES : b * TILES].rearrange("(p j) i -> p j i", j=PACK)
                 nc.sync.dma_start(out=dst, in_=src)
 
         def load_pair(first, pair):
@@ -171,9 +172,14 @@ def tile_moe_res_mlp_relu2_kernel(tc, xT, xr, w1, w2, gate, offs, out):
                 c = wcods.tile([P, H], U32, name="w_codes", align_bytes=64)
                 z = wcods.tile([P, H], U8, name="w_scales", align_bytes=64)
                 codes[e, s], scales[e, s] = c, z
-                for half, cut in enumerate(W_VECTOR_HALVES):
-                    src = raw[e, s][:, half * 2 * H : (half + 1) * 2 * H].rearrange("p (j m t) -> p m j t", t=TILES, j=PACK)
-                    round_groups(dst[:, half * P // 2 : (half + 1) * P // 2], src, cut)
+                cut = LAST_SPLIT * PACK * TILES
+                first = raw[e, s][:, :cut].rearrange("p (j m t) -> p m j t", t=TILES, j=PACK)
+                second = raw[e, s][:, cut:].rearrange("p (j m t) -> p m j t", t=TILES, j=PACK)
+                round_groups(dst[:, :LAST_SPLIT], first, LAST_VECTOR[0])
+                for a, b in ((LAST_SPLIT, P // 2), (P // 2, LAST_VECTOR[1])):
+                    nc.vector.tensor_copy(dst[:, a:b], second[:, a - LAST_SPLIT : b - LAST_SPLIT])
+                nc.scalar.activation(dst[:, LAST_VECTOR[1] :], second[:, LAST_VECTOR[1] - LAST_SPLIT :], COPY)
+                for half in range(2):
                     for t in range(TILES):
                         a = t * P + half * P // 2
                         b = a + P // 2
@@ -212,18 +218,14 @@ def tile_moe_res_mlp_relu2_kernel(tc, xT, xr, w1, w2, gate, offs, out):
             )
 
         def multiply(e, s):
-            if e < LAST:
-                if s < PASSES - 1:
-                    return
+            if s == 0 and e < LAST:
                 sums = psum.tile([P, TILES, C], F32, name="sums", bufs=2)
                 acc[e] = [sums[:, t, :] for t in range(TILES)]
                 whole[e] = sums
-                order = [(t, k) for t in range(TILES) for k in range(PASSES)]
-            else:
-                if s == 0:
-                    tiles = [psum.tile([P, C], F32, name=f"last{t}") for t in range(TILES)]
-                    acc[e] = [tile[:] for tile in tiles]
-                order = [(t, s) for t in range(TILES)]
+            elif s == 0:
+                tiles = [psum.tile([P, C], F32, name=f"last{t}") for t in range(TILES)]
+                acc[e] = [tile[:] for tile in tiles]
+            order = [(t, s) for t in range(TILES)]
             cols = slice(e * C, (e + 1) * C)
             for t, k in order:
                 rows = slice(t * P, (t + 1) * P)
@@ -233,8 +235,8 @@ def tile_moe_res_mlp_relu2_kernel(tc, xT, xr, w1, w2, gate, offs, out):
                     lhsT_scale=scales[e, k][:, rows],
                     rhs=slot_words[k][:, cols].bitcast(FP8X4),
                     rhs_scale=slot_planes[4 * k : P, cols],
-                    start=(k == 0),
-                    stop=(k == PASSES - 1),
+                    start=(k == 0 and (t == 0 or e == LAST)),
+                    stop=(k == PASSES - 1 and (t == TILES - 1 or e == LAST)),
                 )
 
         def rectify(e):
@@ -258,7 +260,9 @@ def tile_moe_res_mlp_relu2_kernel(tc, xT, xr, w1, w2, gate, offs, out):
                 g = w2_raw[W2_LATE][:, : C * TILES // 2].bitcast(BF16)
                 src = last_relu.rearrange("p t (c i) -> p c t i", i=LINE)
                 dst = g.rearrange("p (c i t) -> p c t i", i=LINE, t=TILES)
-                nc.scalar.activation(dst, src, SQUARE)
+                cut = C // LINE // 2
+                nc.vector.tensor_tensor(dst[:, cut:], src[:, cut:], src[:, cut:], MULT)
+                nc.scalar.activation(dst[:, :cut], src[:, :cut], SQUARE)
             hid[e] = g
 
         def quantise_hidden(e):
@@ -269,7 +273,10 @@ def tile_moe_res_mlp_relu2_kernel(tc, xT, xr, w1, w2, gate, offs, out):
 
         def second_product(e):
             c, z = h_mx[e]
-            y = ypsum.tile([P, C], F32, name="y")
+            if e == LAST - 1:
+                y = psum.tile([P, C], F32, name=f"last{TILES - 2}")
+            else:
+                y = ypsum.tile([P, C], F32, name="y")
             cols = slice(e * N, (e + 1) * N)
             nc.tensor.matmul_mx(
                 out=y[:],
@@ -284,7 +291,7 @@ def tile_moe_res_mlp_relu2_kernel(tc, xT, xr, w1, w2, gate, offs, out):
 
         def weigh(e):
             if e < LAST - 1:
-                gated[e] = raw[e + 1, 2][:, PACK * H - C :]
+                gated[e] = raw[e + 1, 2][:, :C]
             else:
                 gated[e] = hids.tile([P, C], F32, name="gated")[:]
             nc.vector.tensor_tensor(gated[e], y_sum[e][:], gates[:, e * C : (e + 1) * C], MULT)
@@ -328,10 +335,10 @@ def tile_moe_res_mlp_relu2_kernel(tc, xT, xr, w1, w2, gate, offs, out):
             if e < LAST:
                 load_third(e + 1)
             round_pass(e, 2)
-            quantise(e, 2)
-            multiply(e, 2)
             if 0 < e < LAST:
                 weigh(e - 1)
+            quantise(e, 2)
+            multiply(e, 2)
             if e in W2_LOADS:
                 round_second(W2_LOADS[e])
                 quantise_second(*W2_LOADS[e][1:])
@@ -339,11 +346,11 @@ def tile_moe_res_mlp_relu2_kernel(tc, xT, xr, w1, w2, gate, offs, out):
                 scatter(e - 1)
         round_second(W2_LATE)
         quantise_second(LAST - 1, LAST)
-        second_product(LAST - 1)
         quantise_second(LAST, E)
         rectify(LAST)
-        weigh(LAST - 1)
+        second_product(LAST - 1)
         square(LAST)
+        weigh(LAST - 1)
         quantise_hidden(LAST)
         second_product(LAST)
         scatter(LAST - 1)

@@ -29,13 +29,17 @@ LAST = E - 1
 
 X_SCALAR = 896
 X_CHUNKS = ((1024, 1280), (0, 512), (512, 1024))
-W_VECTOR = (56, 64, 88)
+W_VECTOR = (32, 64, 80)
+W_VECTOR_FIRST = 72
 W_VECTOR_LAST = (56, 72)
 LAST_SPLIT = 48
 LAST_VECTOR = (32, 104)
-PAIRED = 2
-W2_LOADS = {0: ("w2", 0, 2), 2: ("w2", 2, 4)}
+RUNS = ((0, 3), (3, 5), (5, 7), (7, 9)) + tuple((i, i + 1) for i in range(9, E * PASSES))
+RING = 10
+FRESH = 2
+W2_EARLY = ("w2", 0, 4)
 W2_LATE = ("w2", 4, 6)
+LENT = 32
 OUT_PIECES = ((0, 256), (256, 608), (608, 992), (992, 1280))
 
 
@@ -52,6 +56,8 @@ def tile_moe_res_mlp_relu2_kernel(tc, xT, xr, w1, w2, gate, offs, out):
         ypsum = ctx.enter_context(tc.psum_pool(name="ypsum", bufs=2))
 
         lists = held.tile([P, S // 16], U16, name="lists")
+        gate_rows = held.tile([P, C], F32, name="gate_rows")
+        nc.vector.memset(gate_rows[:], 0.0)
         planes = held.tile([P, T], U8, name="planes", align_bytes=64)
         nc.vector.memset(planes[:], 0)
         window = held.tile([P, T], F32, name="window")
@@ -65,79 +71,63 @@ def tile_moe_res_mlp_relu2_kernel(tc, xT, xr, w1, w2, gate, offs, out):
         w2_grp = held.tile([P, E * N * PACK], BF16, name="w2_grp", align_bytes=64)
         w2_codes = held.tile([P, E * N], U32, name="w2_codes", align_bytes=64)
         w2_scales = held.tile([P, E * N], U8, name="w2_scales", align_bytes=64)
-        gates = held.tile([P, S], F32, name="gates")
-        gate_rows = held.tile([P, C], F32, name="gate_rows")
-        nc.vector.memset(gate_rows[:], 0.0)
+        gates = held.tile([P, S + LENT], F32, name="gates")
+        nc.vector.memset(gates[:, LAST * C : LAST * C + LENT], 1.0)
+        last_sums = held.tile([P, 2 * C], F32, name="last_sums")
         gate_cols = held.tile([P, E], F32, name="gate_cols")
         identity = held.tile([P, P], F32, name="identity")
         make_identity(nc, identity[:])
         result = held.tile([P, T], F32, name="result")
-        pairs = [held.tile([P, 2, PACK * H], F32, name=f"pair{r}", align_bytes=64) for r in range(3)]
-        singles = [held.tile([P, PACK * H], F32, name=f"single{r}", align_bytes=64) for r in range(2)]
-        seconds = [held.tile([P, 2 * PACK * N], F32, name=f"second{r}", align_bytes=64) for r in range(2)]
-
-        raw = {(0, 0): pairs[0][:, 0, :], (0, 1): pairs[0][:, 1, :]}
-        for e in range(LAST):
-            raw[e, 2], raw[e + 1, 0] = (pairs[(e + 1) % len(pairs)][:, half, :] for half in range(2))
-            raw[e + 1, 1] = singles[e % len(singles)][:]
-        raw[LAST, 2] = pairs[0][:, 0, :]
-        xr_raw = pairs[0][:, 1, :T]
-        w2_raw = {item: seconds[r % len(seconds)] for r, item in enumerate(list(W2_LOADS.values()) + [W2_LATE])}
-        last_relu = seconds[1][:, : TILES * C].rearrange("p (t c) -> p t c", t=TILES)
+        WIDE = PACK * H
+        fresh = [held.tile([P, (b - a) * WIDE], F32, name=f"fresh{a}", align_bytes=64) for a, b in RUNS[:FRESH]]
+        early_raw = held.tile([P, 4 * PACK * N], F32, name="early_raw", align_bytes=64)
+        raw = {}
+        w2_raw = {W2_EARLY: early_raw[:]}
+        last_relu = early_raw[:, : TILES * C].rearrange("p (t c) -> p t c", t=TILES)
         x_raw, grp, codes, scales, acc, whole, relu, hid, y_sum, gated = {}, {}, {}, {}, {}, {}, {}, {}, {}, {}
         h_mx = {}
 
         def load_tokens(s):
-            t = xraws.tile([P, PACK, T], F32, name="x_raw")
+            t = xraws.tile([P, PACK, T], F32, name="x_raw", align_bytes=64)
             nc.sync.dma_start(out=t[:], in_=xT[s * K_PASS : (s + 1) * K_PASS, :].rearrange("(p j) t -> p j t", j=PACK))
             x_raw[s] = t
 
-        def load_pass(e, s):
-            rows = w1[e, s * K_PASS : (s + 1) * K_PASS, :]
-            if (e, s) != (LAST, PASSES - 1):
-                nc.sync.dma_start(out=raw[e, s], in_=rows.rearrange("(p j) i -> p (j i)", j=PACK))
-                return
-            for a, b in ((0, LAST_SPLIT), (LAST_SPLIT, P)):
-                dst = raw[e, s][:, a * PACK * TILES : b * PACK * TILES].rearrange("p (j i) -> p j i", j=PACK)
-                src = rows[:, a * TILES : b * TILES].rearrange("(p j) i -> p j i", j=PACK)
-                nc.sync.dma_start(out=dst, in_=src)
-
-        def load_pair(first, pair):
-            rows = w1.rearrange("e k i -> (e k) i")[first * K_PASS : (first + 2) * K_PASS, :]
-            nc.sync.dma_start(out=pair[:], in_=rows.rearrange("(s p j) i -> p s (j i)", s=2, j=PACK))
-
-        def load_third(e):
-            if e < PAIRED:
-                load_pair(e * PASSES + PASSES - 1, pairs[(e + 1) % len(pairs)])
+        def load_run(r):
+            a, b = RUNS[r]
+            if r < FRESH:
+                buf = fresh[r][:]
+            elif r < FRESH + PASSES:
+                buf = xraws.tile([P, (b - a) * WIDE], F32, name="x_raw", align_bytes=64)[:]
             else:
-                load_pass(e, PASSES - 1)
+                buf = raw[divmod(a - RING, PASSES)]
+            for i in range(a, b):
+                raw[divmod(i, PASSES)] = buf[:, (i - a) * WIDE : (i - a + 1) * WIDE]
+            rows = w1.rearrange("e k i -> (e k) i")[a * K_PASS : b * K_PASS, :]
+            if r < len(RUNS) - 1:
+                dst = buf.rearrange("p (s q) -> p s q", s=b - a)
+                nc.sync.dma_start(out=dst, in_=rows.rearrange("(s p j) i -> p s (j i)", s=b - a, j=PACK))
+                return
+            for m, n in ((0, LAST_SPLIT), (LAST_SPLIT, P)):
+                dst = buf[:, m * PACK * TILES : n * PACK * TILES].rearrange("p (j i) -> p j i", j=PACK)
+                src = rows[:, m * TILES : n * TILES].rearrange("(p j) i -> p j i", j=PACK)
+                nc.sync.dma_start(out=dst, in_=src)
 
         def load_second(item):
             a, b = item[1:]
             dst = w2_raw[item][:, : (b - a) * PACK * N].rearrange("p (e q) -> p e q", e=b - a)
             nc.sync.dma_start(out=dst, in_=w2[a:b].rearrange("e (p j) n -> p e (j n)", j=PACK))
 
-        def load_behind_third(e):
-            if e in W2_LOADS:
-                load_second(W2_LOADS[e])
-            if e == LAST:
-                load_second(W2_LATE)
-                nc.sync.dma_start(out=xr_raw, in_=xr)
-                return
-            if e >= PAIRED:
-                load_pass(e + 1, 0)
-            load_pass(e + 1, 1)
-
         def spread_gate():
             turned = psum.tile([P, P], F32, name="last0")
             nc.tensor.transpose(turned[:], gate_rows[:], identity[:])
             nc.scalar.activation(gate_cols[:], turned[:, :E], COPY)
-            for bank, (a, b) in enumerate(((0, TILES), (TILES, E))):
+            for bank, (a, b) in enumerate(((0, TILES), (TILES, LAST), (LAST, E))):
                 wide = psum.tile([P, (b - a) * C], F32, name=f"last{bank + 1}")
                 for e in range(a, b):
                     column = gate_cols[:, e : e + 1].to_broadcast([P, P])
                     nc.tensor.transpose(wide[:, (e - a) * C : (e - a + 1) * C], column, identity[:])
-                nc.scalar.activation(gates[:, a * C : b * C], wide[:], COPY)
+                shift = LENT if a == LAST else 0
+                nc.scalar.activation(gates[:, a * C + shift : b * C + shift], wide[:], COPY)
 
         def tokens(s):
             g = xgrps.tile([P, T, PACK], BF16, name="x_grp", align_bytes=64)
@@ -186,7 +176,7 @@ def tile_moe_res_mlp_relu2_kernel(tc, xT, xr, w1, w2, gate, offs, out):
                         nc.vector.quantize_mx(out=c[:, a:b].bitcast(FP8X4), scales=z[:, a:b], in_=g[:, PACK * a : PACK * b])
                 return
             if e == 0:
-                cut = P if s == 0 else 0
+                cut = W_VECTOR_FIRST
             else:
                 cut = (W_VECTOR_LAST if e == LAST else W_VECTOR)[s]
             round_groups(dst, raw[e, s].rearrange("p (j m t) -> p m j t", t=TILES, j=PACK), cut)
@@ -205,7 +195,7 @@ def tile_moe_res_mlp_relu2_kernel(tc, xT, xr, w1, w2, gate, offs, out):
                 dst = w2_grp[:, e * N * PACK : (e + 1) * N * PACK].rearrange("p (c i j) -> p c j i", i=LINE, j=PACK)
                 src = w2_raw[item][:, (e - a) * N * PACK : (e - a + 1) * N * PACK]
                 src = src.rearrange("p (j c i) -> p c j i", i=LINE, j=PACK)
-                if item == W2_LATE:
+                if item == W2_LATE or e % 2:
                     nc.vector.tensor_copy(dst, src)
                 else:
                     nc.scalar.activation(dst, src, COPY)
@@ -293,29 +283,29 @@ def tile_moe_res_mlp_relu2_kernel(tc, xT, xr, w1, w2, gate, offs, out):
             if e < LAST - 1:
                 gated[e] = raw[e + 1, 2][:, :C]
             else:
-                gated[e] = hids.tile([P, C], F32, name="gated")[:]
+                gated[e] = last_sums[:, :C]
             nc.vector.tensor_tensor(gated[e], y_sum[e][:], gates[:, e * C : (e + 1) * C], MULT)
 
-        def scatter(e, a=0, b=C, second=None):
-            offsets = lists[:, (e * C + a) // 16 : (e * C + b) // 16]
-            nc.vector.tensor_tensor(window[:].indirect(offsets), gated[e][:, a:b], zeros[:, a:b] if second is None else second, ADD)
+        def scatter(e, width=C):
+            offsets = lists[:, e * C // 16 : (e * C + width) // 16]
+            nc.vector.tensor_tensor(window[:].indirect(offsets), gated[e][:, :width], zeros[:, :width], ADD)
 
-        load_tokens(0)
+        load_second(W2_EARLY)
         nc.sync.dma_start(lists[:], offs)
         nc.sync.dma_start(out=gate_rows[:E, :], in_=gate[0].rearrange("(e c) -> e c", e=E))
-        for s in range(1, PASSES):
+        for s in range(PASSES):
             load_tokens(s)
-        load_pair(0, pairs[0])
-        load_third(0)
-        load_behind_third(0)
+        for r in range(FRESH):
+            load_run(r)
+        round_second(W2_EARLY)
+        quantise_second(*W2_EARLY[1:])
+        spread_gate()
         for s in range(PASSES):
             tokens(s)
-            if s == 0:
-                spread_gate()
+        for r in range(FRESH, FRESH + PASSES):
+            load_run(r)
 
         for e in range(E):
-            if e:
-                load_behind_third(e)
             round_pass(e, 0)
             if e:
                 rectify(e - 1)
@@ -332,18 +322,22 @@ def tile_moe_res_mlp_relu2_kernel(tc, xT, xr, w1, w2, gate, offs, out):
                 second_product(e - 1)
             multiply(e, 1)
 
-            if e < LAST:
-                load_third(e + 1)
             round_pass(e, 2)
             if 0 < e < LAST:
                 weigh(e - 1)
             quantise(e, 2)
             multiply(e, 2)
-            if e in W2_LOADS:
-                round_second(W2_LOADS[e])
-                quantise_second(*W2_LOADS[e][1:])
             if 0 < e < LAST:
                 scatter(e - 1)
+            for r, (a, b) in enumerate(RUNS):
+                if a >= RING and (a - RING) // PASSES == e:
+                    load_run(r)
+            if e == (E * PASSES - RING) // PASSES:
+                w2_raw[W2_LATE] = raw[e, 2][:, : 2 * PACK * N]
+                load_second(W2_LATE)
+            if e == (E * PASSES + 1 - RING) // PASSES:
+                xr_raw = raw[e, 0][:, :T]
+                nc.sync.dma_start(out=xr_raw, in_=xr)
         round_second(W2_LATE)
         quantise_second(LAST - 1, LAST)
         quantise_second(LAST, E)
@@ -353,9 +347,10 @@ def tile_moe_res_mlp_relu2_kernel(tc, xT, xr, w1, w2, gate, offs, out):
         weigh(LAST - 1)
         quantise_hidden(LAST)
         second_product(LAST)
-        scatter(LAST - 1)
-        weigh(LAST)
-        scatter(LAST)
+        scatter(LAST - 1, C - LENT)
+        nc.scalar.activation(last_sums[:, C:], y_sum[LAST][:], COPY)
+        offsets = lists[:, (LAST * C - LENT) // 16 :]
+        nc.vector.tensor_tensor(window[:].indirect(offsets), last_sums[:, C - LENT :], gates[:, LAST * C :], MULT)
 
         for a, b in OUT_PIECES:
             nc.vector.tensor_tensor(result[:, a:b], window[:, a:b], xr_raw[:, a:b], ADD)

@@ -33,12 +33,12 @@ W_VECTOR = (32, 64, 80)
 W_VECTOR_FIRST = 72
 W_VECTOR_LAST = (56, 72)
 LAST_SPLIT = 48
-LAST_VECTOR = (32, 104)
+LAST_VECTOR = (32, 100)
 RUNS = ((0, 3), (3, 5), (5, 7), (7, 9)) + tuple((i, i + 1) for i in range(9, E * PASSES))
 RING = 10
 FRESH = 2
 W2_EARLY = ("w2", 0, 4)
-W2_LATE = ("w2", 4, 6)
+W2_LATE = (("w2", 4, 5), ("w2", 5, 6))
 LENT = 32
 OUT_PIECES = ((0, 256), (256, 608), (608, 992), (992, 1280))
 
@@ -195,7 +195,7 @@ def tile_moe_res_mlp_relu2_kernel(tc, xT, xr, w1, w2, gate, offs, out):
                 dst = w2_grp[:, e * N * PACK : (e + 1) * N * PACK].rearrange("p (c i j) -> p c j i", i=LINE, j=PACK)
                 src = w2_raw[item][:, (e - a) * N * PACK : (e - a + 1) * N * PACK]
                 src = src.rearrange("p (j c i) -> p c j i", i=LINE, j=PACK)
-                if item == W2_LATE or e % 2:
+                if e % 2:
                     nc.vector.tensor_copy(dst, src)
                 else:
                     nc.scalar.activation(dst, src, COPY)
@@ -247,7 +247,7 @@ def tile_moe_res_mlp_relu2_kernel(tc, xT, xr, w1, w2, gate, offs, out):
                 g = raw[e + 1, 1][:, : C * TILES // 2].bitcast(BF16)
                 nc.scalar.activation(g.rearrange("p (j q) -> p j q", j=PACK), relu[e], SQUARE)
             else:
-                g = w2_raw[W2_LATE][:, : C * TILES // 2].bitcast(BF16)
+                g = w2_raw[W2_LATE[1]][:, : C * TILES // 2].bitcast(BF16)
                 src = last_relu.rearrange("p t (c i) -> p c t i", i=LINE)
                 dst = g.rearrange("p (c i t) -> p c t i", i=LINE, t=TILES)
                 cut = C // LINE // 2
@@ -333,13 +333,15 @@ def tile_moe_res_mlp_relu2_kernel(tc, xT, xr, w1, w2, gate, offs, out):
                 if a >= RING and (a - RING) // PASSES == e:
                     load_run(r)
             if e == (E * PASSES - RING) // PASSES:
-                w2_raw[W2_LATE] = raw[e, 2][:, : 2 * PACK * N]
-                load_second(W2_LATE)
+                for r, item in enumerate(W2_LATE):
+                    w2_raw[item] = raw[e, 2][:, r * PACK * N : (r + 1) * PACK * N]
+                    load_second(item)
             if e == (E * PASSES + 1 - RING) // PASSES:
                 xr_raw = raw[e, 0][:, :T]
                 nc.sync.dma_start(out=xr_raw, in_=xr)
-        round_second(W2_LATE)
+        round_second(W2_LATE[0])
         quantise_second(LAST - 1, LAST)
+        round_second(W2_LATE[1])
         quantise_second(LAST, E)
         rectify(LAST)
         second_product(LAST - 1)

@@ -26,19 +26,16 @@ PASSES = K // K_PASS
 TILES = H // P
 LINE = 4
 LAST = E - 1
+WIDE = PACK * H
+GROUP = PACK * TILES
 
-X_SCALAR = 896
+X_RUNS = ((0, 2), (2, 3))
+X_SCALAR = 832
 X_CHUNKS = ((1024, 1280), (0, 512), (512, 1024))
-W_VECTOR = (32, 64, 80)
-W_VECTOR_FIRST = 72
-W_VECTOR_LAST = (56, 72)
-LAST_SPLIT = 48
-LAST_VECTOR = (32, 100)
-RUNS = ((0, 3), (3, 5), (5, 7), (7, 9)) + tuple((i, i + 1) for i in range(9, E * PASSES))
-RING = 10
-FRESH = 2
-W2_EARLY = ("w2", 0, 4)
-W2_LATE = (("w2", 4, 5), ("w2", 5, 6))
+RUNS = (3, 3, 2, 2, 2, 1, 1, 1, 1, 1, 1)
+SHARES = ((72, 72, 72), (48, 72, 96), (32, 76, 80), (48, 76, 80), (32, 76, 80), (56, 72, 32, 100))
+CUT = 48
+EARLY = 4
 LENT = 32
 OUT_PIECES = ((0, 256), (256, 608), (608, 992), (992, 1280))
 
@@ -47,13 +44,11 @@ def tile_moe_res_mlp_relu2_kernel(tc, xT, xr, w1, w2, gate, offs, out):
     nc = tc.nc
     with ExitStack() as ctx:
         held = ctx.enter_context(tc.tile_pool(name="held", bufs=1))
-        xraws = ctx.enter_context(tc.tile_pool(name="xraws", bufs=PASSES))
         xgrps = ctx.enter_context(tc.tile_pool(name="xgrps", bufs=2))
         wgrps = ctx.enter_context(tc.tile_pool(name="wgrps", bufs=3))
-        wcods = ctx.enter_context(tc.tile_pool(name="wcods", bufs=2 * PASSES))
+        wcods = ctx.enter_context(tc.tile_pool(name="wcods", bufs=6))
         hids = ctx.enter_context(tc.tile_pool(name="hids", bufs=2))
         psum = ctx.enter_context(tc.psum_pool(name="psum", bufs=1))
-        ypsum = ctx.enter_context(tc.psum_pool(name="ypsum", bufs=2))
 
         lists = held.tile([P, S // 16], U16, name="lists")
         gate_rows = held.tile([P, C], F32, name="gate_rows")
@@ -64,58 +59,48 @@ def tile_moe_res_mlp_relu2_kernel(tc, xT, xr, w1, w2, gate, offs, out):
         nc.vector.memset(window[:], 0.0)
         zeros = held.tile([P, C], F32, name="zeros")
         nc.vector.memset(zeros[:], 0.0)
-
+        gates = held.tile([P, S + LENT], F32, name="gates")
+        nc.vector.memset(gates[:, LAST * C : LAST * C + LENT], 1.0)
+        identity = held.tile([P, P], F32, name="identity")
+        make_identity(nc, identity[:])
+        gate_cols = held.tile([P, E], F32, name="gate_cols")
         words = [held.tile([P, T], U32, name=f"words{s}", align_bytes=64) for s in range(PASSES)]
         slot_words = [held.tile([P, S], U32, name=f"slot_words{s}", align_bytes=64) for s in range(PASSES)]
         slot_planes = held.tile([P, S], U8, name="slot_planes", align_bytes=64)
+        early_raw = held.tile([P, EARLY * PACK * N], F32, name="early_raw", align_bytes=64)
+        w2_raw = {}
         w2_grp = held.tile([P, E * N * PACK], BF16, name="w2_grp", align_bytes=64)
         w2_codes = held.tile([P, E * N], U32, name="w2_codes", align_bytes=64)
         w2_scales = held.tile([P, E * N], U8, name="w2_scales", align_bytes=64)
-        gates = held.tile([P, S + LENT], F32, name="gates")
-        nc.vector.memset(gates[:, LAST * C : LAST * C + LENT], 1.0)
         last_sums = held.tile([P, 2 * C], F32, name="last_sums")
-        gate_cols = held.tile([P, E], F32, name="gate_cols")
-        identity = held.tile([P, P], F32, name="identity")
-        make_identity(nc, identity[:])
         result = held.tile([P, T], F32, name="result")
-        WIDE = PACK * H
-        fresh = [held.tile([P, (b - a) * WIDE], F32, name=f"fresh{a}", align_bytes=64) for a, b in RUNS[:FRESH]]
-        early_raw = held.tile([P, 4 * PACK * N], F32, name="early_raw", align_bytes=64)
-        raw = {}
-        w2_raw = {W2_EARLY: early_raw[:]}
-        last_relu = early_raw[:, : TILES * C].rearrange("p (t c) -> p t c", t=TILES)
-        x_raw, grp, codes, scales, acc, whole, relu, hid, y_sum, gated = {}, {}, {}, {}, {}, {}, {}, {}, {}, {}
-        h_mx = {}
+        x_buf = held.tile([P, PASSES * PACK * T], F32, name="x_buf", align_bytes=64)
+        x_raw, raw, codes, scales, sums, y_sum, gated, hid, grp, relu = {}, {}, {}, {}, {}, {}, {}, {}, {}, {}
 
-        def load_tokens(s):
-            t = xraws.tile([P, PACK, T], F32, name="x_raw", align_bytes=64)
-            nc.sync.dma_start(out=t[:], in_=xT[s * K_PASS : (s + 1) * K_PASS, :].rearrange("(p j) t -> p j t", j=PACK))
-            x_raw[s] = t
-
-        def load_run(r):
-            a, b = RUNS[r]
-            if r < FRESH:
-                buf = fresh[r][:]
-            elif r < FRESH + PASSES:
-                buf = xraws.tile([P, (b - a) * WIDE], F32, name="x_raw", align_bytes=64)[:]
-            else:
-                buf = raw[divmod(a - RING, PASSES)]
-            for i in range(a, b):
-                raw[divmod(i, PASSES)] = buf[:, (i - a) * WIDE : (i - a + 1) * WIDE]
-            rows = w1.rearrange("e k i -> (e k) i")[a * K_PASS : b * K_PASS, :]
-            if r < len(RUNS) - 1:
-                dst = buf.rearrange("p (s q) -> p s q", s=b - a)
-                nc.sync.dma_start(out=dst, in_=rows.rearrange("(s p j) i -> p s (j i)", s=b - a, j=PACK))
-                return
-            for m, n in ((0, LAST_SPLIT), (LAST_SPLIT, P)):
-                dst = buf[:, m * PACK * TILES : n * PACK * TILES].rearrange("p (j i) -> p j i", j=PACK)
-                src = rows[:, m * TILES : n * TILES].rearrange("(p j) i -> p j i", j=PACK)
-                nc.sync.dma_start(out=dst, in_=src)
-
-        def load_second(item):
-            a, b = item[1:]
-            dst = w2_raw[item][:, : (b - a) * PACK * N].rearrange("p (e q) -> p e q", e=b - a)
+        def load_second(a, b, buf):
+            for e in range(a, b):
+                w2_raw[e] = buf[:, (e - a) * PACK * N : (e - a + 1) * PACK * N]
+            dst = buf[:, : (b - a) * PACK * N].rearrange("p (e q) -> p e q", e=b - a)
             nc.sync.dma_start(out=dst, in_=w2[a:b].rearrange("e (p j) n -> p e (j n)", j=PACK))
+
+        def load_tokens(a, b):
+            t = x_buf[:, a * PACK * T : b * PACK * T]
+            src = xT[a * K_PASS : b * K_PASS, :].rearrange("(s p j) t -> p s (j t)", s=b - a, j=PACK)
+            nc.sync.dma_start(out=t.rearrange("p (s q) -> p s q", s=b - a), in_=src)
+            for s in range(a, b):
+                x_raw[s] = t[:, (s - a) * PACK * T : (s - a + 1) * PACK * T]
+
+        def load_run(first, count, buf):
+            rows = w1.rearrange("e k i -> (e k) i")[first * K_PASS : (first + count) * K_PASS, :]
+            for i in range(count):
+                raw[first + i] = buf[:, i * WIDE : (i + 1) * WIDE]
+            if first + count < E * PASSES:
+                dst = buf[:, : count * WIDE].rearrange("p (s q) -> p s q", s=count)
+                nc.sync.dma_start(out=dst, in_=rows.rearrange("(s p j) i -> p s (j i)", s=count, j=PACK))
+                return
+            for m, n in ((0, CUT), (CUT, P)):
+                dst = buf[:, m * GROUP : n * GROUP].rearrange("p (j i) -> p j i", j=PACK)
+                nc.sync.dma_start(out=dst, in_=rows[:, m * TILES : n * TILES].rearrange("(p j) i -> p j i", j=PACK))
 
         def spread_gate():
             turned = psum.tile([P, P], F32, name="last0")
@@ -129,10 +114,25 @@ def tile_moe_res_mlp_relu2_kernel(tc, xT, xr, w1, w2, gate, offs, out):
                 shift = LENT if a == LAST else 0
                 nc.scalar.activation(gates[:, a * C + shift : b * C + shift], wide[:], COPY)
 
+        def round_second(e, engine):
+            dst = w2_grp[:, e * N * PACK : (e + 1) * N * PACK].rearrange("p (c i j) -> p c j i", i=LINE, j=PACK)
+            src = w2_raw[e].rearrange("p (j c i) -> p c j i", i=LINE, j=PACK)
+            if engine == "vector":
+                nc.vector.tensor_copy(dst, src)
+            else:
+                nc.scalar.activation(dst, src, COPY)
+
+        def quantise_second(a, b):
+            nc.vector.quantize_mx(
+                out=w2_codes[:, a * N : b * N].bitcast(FP8X4),
+                scales=w2_scales[:, a * N : b * N],
+                in_=w2_grp[:, PACK * a * N : PACK * b * N],
+            )
+
         def tokens(s):
             g = xgrps.tile([P, T, PACK], BF16, name="x_grp", align_bytes=64)
             dst = g[:].rearrange("p (c i) j -> p c j i", i=LINE)
-            src = x_raw[s][:].rearrange("p j (c i) -> p c j i", i=LINE)
+            src = x_raw[s].rearrange("p (j c i) -> p c j i", i=LINE, j=PACK)
             first_chunk = X_CHUNKS[1][1]
             for a, b in ((0, first_chunk), (first_chunk, X_SCALAR)):
                 nc.scalar.activation(dst[:, a // LINE : b // LINE], src[:, a // LINE : b // LINE], COPY)
@@ -148,112 +148,78 @@ def tile_moe_res_mlp_relu2_kernel(tc, xT, xr, w1, w2, gate, offs, out):
             if s == PASSES - 1:
                 nc.vector.tensor_copy(slot_planes[:], planes[:].indirect(lists[:]))
 
-        def round_groups(dst, src, cut):
-            if cut:
-                nc.vector.tensor_copy(dst[:, :cut], src[:, :cut])
-            if cut < P:
-                nc.scalar.activation(dst[:, cut:], src[:, cut:], COPY)
-
         def round_pass(e, s):
             g = wgrps.tile([P, H * PACK], BF16, name="w_grp", align_bytes=64)
             grp[e, s] = g
             dst = g[:].rearrange("p (t m j) -> p m j t", t=TILES, j=PACK)
-            if (e, s) == (LAST, PASSES - 1):
-                c = wcods.tile([P, H], U32, name="w_codes", align_bytes=64)
-                z = wcods.tile([P, H], U8, name="w_scales", align_bytes=64)
-                codes[e, s], scales[e, s] = c, z
-                cut = LAST_SPLIT * PACK * TILES
-                first = raw[e, s][:, :cut].rearrange("p (j m t) -> p m j t", t=TILES, j=PACK)
-                second = raw[e, s][:, cut:].rearrange("p (j m t) -> p m j t", t=TILES, j=PACK)
-                round_groups(dst[:, :LAST_SPLIT], first, LAST_VECTOR[0])
-                for a, b in ((LAST_SPLIT, P // 2), (P // 2, LAST_VECTOR[1])):
-                    nc.vector.tensor_copy(dst[:, a:b], second[:, a - LAST_SPLIT : b - LAST_SPLIT])
-                nc.scalar.activation(dst[:, LAST_VECTOR[1] :], second[:, LAST_VECTOR[1] - LAST_SPLIT :], COPY)
-                for half in range(2):
-                    for t in range(TILES):
-                        a = t * P + half * P // 2
-                        b = a + P // 2
-                        nc.vector.quantize_mx(out=c[:, a:b].bitcast(FP8X4), scales=z[:, a:b], in_=g[:, PACK * a : PACK * b])
-                return
-            if e == 0:
-                cut = W_VECTOR_FIRST
-            else:
-                cut = (W_VECTOR_LAST if e == LAST else W_VECTOR)[s]
-            round_groups(dst, raw[e, s].rearrange("p (j m t) -> p m j t", t=TILES, j=PACK), cut)
+            buf = raw[e * PASSES + s]
+            pieces = ((0, P),) if (e, s) != (LAST, PASSES - 1) else ((0, CUT), (CUT, P))
+            for (m, n), cut in zip(pieces, SHARES[e][s:]):
+                src = buf[:, m * GROUP : n * GROUP].rearrange("p (j m t) -> p m j t", t=TILES, j=PACK)
+                mid = P // 2 if m < P // 2 < cut and m else m
+                if mid > m:
+                    nc.vector.tensor_copy(dst[:, m:mid], src[:, : mid - m])
+                nc.vector.tensor_copy(dst[:, mid:cut], src[:, mid - m : cut - m])
+                nc.scalar.activation(dst[:, cut:n], src[:, cut - m :], COPY)
 
         def quantise(e, s):
-            if (e, s) == (LAST, PASSES - 1):
-                return
             c = wcods.tile([P, H], U32, name="w_codes", align_bytes=64)
             z = wcods.tile([P, H], U8, name="w_scales", align_bytes=64)
-            nc.vector.quantize_mx(out=c[:].bitcast(FP8X4), scales=z[:], in_=grp[e, s][:])
             codes[e, s], scales[e, s] = c, z
-
-        def round_second(item):
-            a, b = item[1:]
-            for e in range(a, b):
-                dst = w2_grp[:, e * N * PACK : (e + 1) * N * PACK].rearrange("p (c i j) -> p c j i", i=LINE, j=PACK)
-                src = w2_raw[item][:, (e - a) * N * PACK : (e - a + 1) * N * PACK]
-                src = src.rearrange("p (j c i) -> p c j i", i=LINE, j=PACK)
-                if e % 2:
-                    nc.vector.tensor_copy(dst, src)
-                else:
-                    nc.scalar.activation(dst, src, COPY)
-
-        def quantise_second(a, b):
-            nc.vector.quantize_mx(
-                out=w2_codes[:, a * N : b * N].bitcast(FP8X4),
-                scales=w2_scales[:, a * N : b * N],
-                in_=w2_grp[:, PACK * a * N : PACK * b * N],
-            )
+            calls = ((0, H),)
+            if (e, s) == (LAST, PASSES - 1):
+                calls = [(t * P + h * P // 2, t * P + (h + 1) * P // 2) for h in range(2) for t in range(TILES)]
+            for a, b in calls:
+                nc.vector.quantize_mx(
+                    out=c[:, a:b].bitcast(FP8X4), scales=z[:, a:b], in_=grp[e, s][:, PACK * a : PACK * b]
+                )
 
         def multiply(e, s):
             if s == 0 and e < LAST:
-                sums = psum.tile([P, TILES, C], F32, name="sums", bufs=2)
-                acc[e] = [sums[:, t, :] for t in range(TILES)]
-                whole[e] = sums
+                bank = psum.tile([P, TILES, C], F32, name="sums", bufs=2)
+                sums[e] = bank
             elif s == 0:
-                tiles = [psum.tile([P, C], F32, name=f"last{t}") for t in range(TILES)]
-                acc[e] = [tile[:] for tile in tiles]
-            order = [(t, s) for t in range(TILES)]
+                sums[e] = [psum.tile([P, C], F32, name=f"last{t}") for t in range(TILES)]
             cols = slice(e * C, (e + 1) * C)
-            for t, k in order:
+            for t in range(TILES):
                 rows = slice(t * P, (t + 1) * P)
                 nc.tensor.matmul_mx(
-                    out=acc[e][t],
-                    lhsT=codes[e, k][:, rows].bitcast(FP8X4),
-                    lhsT_scale=scales[e, k][:, rows],
-                    rhs=slot_words[k][:, cols].bitcast(FP8X4),
-                    rhs_scale=slot_planes[4 * k : P, cols],
-                    start=(k == 0 and (t == 0 or e == LAST)),
-                    stop=(k == PASSES - 1 and (t == TILES - 1 or e == LAST)),
+                    out=sums[e][t][:] if e == LAST else sums[e][:, t, :],
+                    lhsT=codes[e, s][:, rows].bitcast(FP8X4),
+                    lhsT_scale=scales[e, s][:, rows],
+                    rhs=slot_words[s][:, cols].bitcast(FP8X4),
+                    rhs_scale=slot_planes[4 * s : P, cols],
+                    start=(s == 0 and (t == 0 or e == LAST)),
+                    stop=(s == PASSES - 1 and (t == TILES - 1 or e == LAST)),
                 )
 
         def rectify(e):
             if e < LAST:
-                r = raw[e + 1, 0].rearrange("p (j h) -> p j h", j=PACK)[:, :, :C]
+                r = raw[(e + 1) * PASSES].rearrange("p (j h) -> p j h", j=PACK)[:, :, :C]
                 nc.scalar.activation(
                     r.rearrange("p j (c t) -> p j c t", t=TILES),
-                    whole[e][:].rearrange("p t (j c) -> p j c t", j=PACK),
+                    sums[e][:].rearrange("p t (j c) -> p j c t", j=PACK),
                     RELU,
                 )
                 relu[e] = r
-            else:
-                for t in range(TILES):
-                    nc.scalar.activation(last_relu[:, t, :], acc[e][t], RELU)
+                return
+            relu[e] = early_raw[:, : TILES * C]
+            for t in range(TILES):
+                nc.scalar.activation(relu[e][:, t * C : (t + 1) * C], sums[e][t][:], RELU)
 
         def square(e):
             if e < LAST:
-                g = raw[e + 1, 1][:, : C * TILES // 2].bitcast(BF16)
-                nc.scalar.activation(g.rearrange("p (j q) -> p j q", j=PACK), relu[e], SQUARE)
-            else:
-                g = w2_raw[W2_LATE[1]][:, : C * TILES // 2].bitcast(BF16)
-                src = last_relu.rearrange("p t (c i) -> p c t i", i=LINE)
-                dst = g.rearrange("p (c i t) -> p c t i", i=LINE, t=TILES)
-                cut = C // LINE // 2
-                nc.vector.tensor_tensor(dst[:, cut:], src[:, cut:], src[:, cut:], MULT)
-                nc.scalar.activation(dst[:, :cut], src[:, :cut], SQUARE)
-            hid[e] = g
+                hid[e] = raw[(e + 1) * PASSES + 1][:, : C * TILES // 2].bitcast(BF16)
+                nc.scalar.activation(hid[e].rearrange("p (j q) -> p j q", j=PACK), relu[e], SQUARE)
+                return
+            hid[e] = w2_raw[LAST][:, : C * TILES // 2].bitcast(BF16)
+            src = relu[e].rearrange("p (t c i) -> p c t i", t=TILES, i=LINE)
+            dst = hid[e].rearrange("p (c i t) -> p c t i", i=LINE, t=TILES)
+            cut = C // LINE // 2
+            nc.vector.tensor_tensor(dst[:, cut:], src[:, cut:], src[:, cut:], MULT)
+            nc.scalar.activation(dst[:, :cut], src[:, :cut], SQUARE)
+
+        h_mx = {}
 
         def quantise_hidden(e):
             c = hids.tile([P, C], U32, name="h_codes", align_bytes=64)
@@ -266,7 +232,7 @@ def tile_moe_res_mlp_relu2_kernel(tc, xT, xr, w1, w2, gate, offs, out):
             if e == LAST - 1:
                 y = psum.tile([P, C], F32, name=f"last{TILES - 2}")
             else:
-                y = ypsum.tile([P, C], F32, name="y")
+                y = psum.tile([P, C], F32, name="y", bufs=2)
             cols = slice(e * N, (e + 1) * N)
             nc.tensor.matmul_mx(
                 out=y[:],
@@ -281,7 +247,7 @@ def tile_moe_res_mlp_relu2_kernel(tc, xT, xr, w1, w2, gate, offs, out):
 
         def weigh(e):
             if e < LAST - 1:
-                gated[e] = raw[e + 1, 2][:, :C]
+                gated[e] = raw[(e + 2) * PASSES - 1][:, :C]
             else:
                 gated[e] = last_sums[:, :C]
             nc.vector.tensor_tensor(gated[e], y_sum[e][:], gates[:, e * C : (e + 1) * C], MULT)
@@ -290,20 +256,24 @@ def tile_moe_res_mlp_relu2_kernel(tc, xT, xr, w1, w2, gate, offs, out):
             offsets = lists[:, e * C // 16 : (e * C + width) // 16]
             nc.vector.tensor_tensor(window[:].indirect(offsets), gated[e][:, :width], zeros[:, :width], ADD)
 
-        load_second(W2_EARLY)
+        load_second(0, EARLY, early_raw[:])
         nc.sync.dma_start(lists[:], offs)
         nc.sync.dma_start(out=gate_rows[:E, :], in_=gate[0].rearrange("(e c) -> e c", e=E))
-        for s in range(PASSES):
-            load_tokens(s)
-        for r in range(FRESH):
-            load_run(r)
-        round_second(W2_EARLY)
-        quantise_second(*W2_EARLY[1:])
+        for a, b in X_RUNS:
+            load_tokens(a, b)
+        starts = [sum(RUNS[:r]) for r in range(len(RUNS))]
+        fresh = [held.tile([P, RUNS[r] * WIDE], F32, name=f"fresh{r}", align_bytes=64) for r in range(2)]
+        for r in range(2):
+            load_run(starts[r], RUNS[r], fresh[r][:])
+        for e in range(EARLY):
+            round_second(e, "vector" if e % 2 else "scalar")
+        quantise_second(0, EARLY)
         spread_gate()
         for s in range(PASSES):
             tokens(s)
-        for r in range(FRESH, FRESH + PASSES):
-            load_run(r)
+        reused = held.tile([P, sum(RUNS[2:5]) * WIDE], F32, name="x_buf", align_bytes=64)
+        for r in range(2, 5):
+            load_run(starts[r], RUNS[r], reused[:, (starts[r] - starts[2]) * WIDE :])
 
         for e in range(E):
             round_pass(e, 0)
@@ -311,37 +281,34 @@ def tile_moe_res_mlp_relu2_kernel(tc, xT, xr, w1, w2, gate, offs, out):
                 rectify(e - 1)
             quantise(e, 0)
             multiply(e, 0)
-
             round_pass(e, 1)
             if e:
                 square(e - 1)
             quantise(e, 1)
             if e:
                 quantise_hidden(e - 1)
-            if 0 < e < LAST:
+            if 0 < e <= EARLY:
                 second_product(e - 1)
             multiply(e, 1)
-
             round_pass(e, 2)
-            if 0 < e < LAST:
+            if 0 < e <= EARLY:
                 weigh(e - 1)
             quantise(e, 2)
             multiply(e, 2)
-            if 0 < e < LAST:
+            if 0 < e <= EARLY:
                 scatter(e - 1)
-            for r, (a, b) in enumerate(RUNS):
-                if a >= RING and (a - RING) // PASSES == e:
-                    load_run(r)
-            if e == (E * PASSES - RING) // PASSES:
-                for r, item in enumerate(W2_LATE):
-                    w2_raw[item] = raw[e, 2][:, r * PACK * N : (r + 1) * PACK * N]
-                    load_second(item)
-            if e == (E * PASSES + 1 - RING) // PASSES:
-                xr_raw = raw[e, 0][:, :T]
-                nc.sync.dma_start(out=xr_raw, in_=xr)
-        round_second(W2_LATE[0])
+            for i in range(e * PASSES, (e + 1) * PASSES):
+                if i < len(RUNS) - 5:
+                    load_run(starts[5 + i], RUNS[5 + i], raw[i])
+                if i == len(RUNS) - 5:
+                    load_second(LAST - 1, LAST, raw[i][:, : PACK * N])
+                    load_second(LAST, E, raw[i][:, PACK * N :])
+                if i == len(RUNS) - 4:
+                    residual = raw[i][:, :T]
+                    nc.sync.dma_start(out=residual, in_=xr)
+        round_second(LAST - 1, "scalar")
         quantise_second(LAST - 1, LAST)
-        round_second(W2_LATE[1])
+        round_second(LAST, "vector")
         quantise_second(LAST, E)
         rectify(LAST)
         second_product(LAST - 1)
@@ -353,7 +320,6 @@ def tile_moe_res_mlp_relu2_kernel(tc, xT, xr, w1, w2, gate, offs, out):
         nc.scalar.activation(last_sums[:, C:], y_sum[LAST][:], COPY)
         offsets = lists[:, (LAST * C - LENT) // 16 :]
         nc.vector.tensor_tensor(window[:].indirect(offsets), last_sums[:, C - LENT :], gates[:, LAST * C :], MULT)
-
         for a, b in OUT_PIECES:
-            nc.vector.tensor_tensor(result[:, a:b], window[:, a:b], xr_raw[:, a:b], ADD)
+            nc.vector.tensor_tensor(result[:, a:b], window[:, a:b], residual[:, a:b], ADD)
             nc.sync.dma_start(out=out[:, a:b], in_=result[:, a:b])

@@ -37,6 +37,7 @@ SHARES = ((72, 72, 72), (48, 72, 96), (32, 76, 80), (48, 76, 80), (32, 76, 80), 
 CUT = 48
 EARLY = 4
 LENT = 32
+WARM_UP = (512, 256, 128)
 OUT_PIECES = ((0, 256), (256, 608), (608, 992), (992, 1280))
 
 
@@ -193,6 +194,20 @@ def tile_moe_res_mlp_relu2_kernel(tc, xT, xr, w1, w2, gate, offs, out):
                     stop=(s == PASSES - 1 and (t == TILES - 1 or e == LAST)),
                 )
 
+        def warm_up():
+            spare = psum.tile([P, H], F32, name="y", bufs=2)
+            c, z = codes[LAST, 0], scales[LAST, 0]
+            for width in WARM_UP:
+                nc.tensor.matmul_mx(
+                    out=spare[:, :width],
+                    lhsT=c[:, H - P :].bitcast(FP8X4),
+                    lhsT_scale=z[:, H - P :],
+                    rhs=c[:, :width].bitcast(FP8X4),
+                    rhs_scale=z[:, :width],
+                    start=True,
+                    stop=True,
+                )
+
         def rectify(e):
             if e < LAST:
                 r = raw[(e + 1) * PASSES].rearrange("p (j h) -> p j h", j=PACK)[:, :, :C]
@@ -281,6 +296,8 @@ def tile_moe_res_mlp_relu2_kernel(tc, xT, xr, w1, w2, gate, offs, out):
                 rectify(e - 1)
             quantise(e, 0)
             multiply(e, 0)
+            if e == LAST:
+                warm_up()
             round_pass(e, 1)
             if e:
                 square(e - 1)

@@ -33,10 +33,11 @@ X_RUNS = ((0, 2), (2, 3))
 X_SCALAR = 832
 X_CHUNKS = ((1024, 1280), (0, 512), (512, 1024))
 RUNS = (3, 3, 2, 2, 2, 1, 1, 1, 1, 1, 1)
-SHARES = ((72, 72, 72), (48, 72, 96), (32, 76, 80), (48, 76, 80), (32, 76, 80), (56, 72, 32, 100))
-CUT = 48
+SHARES = ((72, 72, 72), (48, 72, 96), (32, 76, 80), (48, 76, 80), (32, 76, 80), (88, 80, 16, 104))
+CUT = 60
 EARLY = 4
 LENT = 32
+SCATTERS = ((0, 128), (128, 256), (256, 352), (352, 512))
 WARM_UP = (512, 256, 128)
 OUT_PIECES = ((0, 256), (256, 608), (608, 992), (992, 1280))
 
@@ -195,7 +196,7 @@ def tile_moe_res_mlp_relu2_kernel(tc, xT, xr, w1, w2, gate, offs, out):
                 )
 
         def warm_up():
-            spare = psum.tile([P, H], F32, name="y", bufs=2)
+            spare = psum.tile([P, H], F32, name="y")
             c, z = codes[LAST, 0], scales[LAST, 0]
             for width in WARM_UP:
                 nc.tensor.matmul_mx(
@@ -224,7 +225,11 @@ def tile_moe_res_mlp_relu2_kernel(tc, xT, xr, w1, w2, gate, offs, out):
 
         def square(e):
             if e < LAST:
-                hid[e] = raw[(e + 1) * PASSES + 1][:, : C * TILES // 2].bitcast(BF16)
+                if e < LAST - 1:
+                    hid[e] = raw[(e + 1) * PASSES + 1][:, : C * TILES // 2].bitcast(BF16)
+                else:
+                    end = CUT * GROUP + (P // 2 - CUT) * TILES
+                    hid[e] = raw[E * PASSES - 1][:, end - C * TILES // 2 : end].bitcast(BF16)
                 nc.scalar.activation(hid[e].rearrange("p (j q) -> p j q", j=PACK), relu[e], SQUARE)
                 return
             hid[e] = w2_raw[LAST][:, : C * TILES // 2].bitcast(BF16)
@@ -244,13 +249,14 @@ def tile_moe_res_mlp_relu2_kernel(tc, xT, xr, w1, w2, gate, offs, out):
 
         def second_product(e):
             c, z = h_mx[e]
-            if e == LAST - 1:
-                y = psum.tile([P, C], F32, name=f"last{TILES - 2}")
+            if e < EARLY:
+                y = early_sums[:, e * C : (e + 1) * C]
             else:
-                y = psum.tile([P, C], F32, name="y", bufs=2)
+                bank = psum.tile([P, C], F32, name="y" if e == LAST else f"last{TILES - 2}")
+                y = bank[:]
             cols = slice(e * N, (e + 1) * N)
             nc.tensor.matmul_mx(
-                out=y[:],
+                out=y,
                 lhsT=w2_codes[:, cols].bitcast(FP8X4),
                 lhsT_scale=w2_scales[:, cols],
                 rhs=c[:].bitcast(FP8X4),
@@ -261,16 +267,19 @@ def tile_moe_res_mlp_relu2_kernel(tc, xT, xr, w1, w2, gate, offs, out):
             y_sum[e] = y
 
         def weigh(e):
-            if e < LAST - 1:
-                gated[e] = raw[(e + 2) * PASSES - 1][:, :C]
+            a, b = SCATTERS[e]
+            gated[e] = raw[(e + 2) * PASSES - 1][:, : b - a]
+            nc.vector.tensor_tensor(gated[e], early_sums[:, a:b], gates[:, a:b], MULT)
+
+        def scatter(e):
+            a, b = SCATTERS[e]
+            target = window[:].indirect(lists[:, a // 16 : b // 16])
+            if e < EARLY - 1:
+                nc.vector.tensor_tensor(target, gated[e], zeros[:, : b - a], ADD)
             else:
-                gated[e] = last_sums[:, :C]
-            nc.vector.tensor_tensor(gated[e], y_sum[e][:], gates[:, e * C : (e + 1) * C], MULT)
+                nc.scalar.activation(target, gated[e], COPY)
 
-        def scatter(e, width=C):
-            offsets = lists[:, e * C // 16 : (e * C + width) // 16]
-            nc.vector.tensor_tensor(window[:].indirect(offsets), gated[e][:, :width], zeros[:, :width], ADD)
-
+        early_sums = psum.tile([P, EARLY * C], F32, name="early_sums")
         load_second(0, EARLY, early_raw[:])
         nc.sync.dma_start(lists[:], offs)
         nc.sync.dma_start(out=gate_rows[:E, :], in_=gate[0].rearrange("(e c) -> e c", e=E))
@@ -299,15 +308,17 @@ def tile_moe_res_mlp_relu2_kernel(tc, xT, xr, w1, w2, gate, offs, out):
             if e == LAST:
                 warm_up()
             round_pass(e, 1)
-            if e:
+            if 0 < e < LAST:
                 square(e - 1)
             quantise(e, 1)
-            if e:
+            if 0 < e < LAST:
                 quantise_hidden(e - 1)
             if 0 < e <= EARLY:
                 second_product(e - 1)
             multiply(e, 1)
             round_pass(e, 2)
+            if e == LAST:
+                square(e - 1)
             if 0 < e <= EARLY:
                 weigh(e - 1)
             quantise(e, 2)
@@ -323,18 +334,21 @@ def tile_moe_res_mlp_relu2_kernel(tc, xT, xr, w1, w2, gate, offs, out):
                 if i == len(RUNS) - 4:
                     residual = raw[i][:, :T]
                     nc.sync.dma_start(out=residual, in_=xr)
+        quantise_hidden(LAST - 1)
         round_second(LAST - 1, "scalar")
-        quantise_second(LAST - 1, LAST)
         round_second(LAST, "vector")
+        quantise_second(LAST - 1, LAST)
         quantise_second(LAST, E)
         rectify(LAST)
         second_product(LAST - 1)
         square(LAST)
-        weigh(LAST - 1)
+        a = (LAST - 1) * C
+        nc.vector.tensor_tensor(last_sums[:, :C], y_sum[LAST - 1], gates[:, a : a + C], MULT)
         quantise_hidden(LAST)
         second_product(LAST)
-        scatter(LAST - 1, C - LENT)
-        nc.scalar.activation(last_sums[:, C:], y_sum[LAST][:], COPY)
+        offsets = lists[:, a // 16 : (a + C - LENT) // 16]
+        nc.vector.tensor_tensor(window[:].indirect(offsets), last_sums[:, : C - LENT], zeros[:, : C - LENT], ADD)
+        nc.scalar.activation(last_sums[:, C:], y_sum[LAST], COPY)
         offsets = lists[:, (LAST * C - LENT) // 16 :]
         nc.vector.tensor_tensor(window[:].indirect(offsets), last_sums[:, C - LENT :], gates[:, LAST * C :], MULT)
         for a, b in OUT_PIECES:

from contextlib import ExitStack

import concourse.mybir as mybir
from concourse.masks import make_identity

K, T, E, C, H, N = 1536, 1280, 6, 128, 512, 128
S = E * C
FLOPS = 2 * S * (K * H + H * N)

F32 = mybir.dt.float32
BF16 = mybir.dt.bfloat16
U32 = mybir.dt.uint32
U16 = mybir.dt.uint16
U8 = mybir.dt.uint8
FP8X4 = mybir.dt.float8_e4m3fn_x4
COPY = mybir.ActivationFunctionType.Copy
RELU = mybir.ActivationFunctionType.Relu
SQUARE = mybir.ActivationFunctionType.Square
MULT = mybir.AluOpType.mult
ADD = mybir.AluOpType.add

P = 128
PACK = 4
K_PASS = P * PACK
PASSES = K // K_PASS
TILES = H // P
LINE = 4
LAST = E - 1
WIDE = PACK * H
GROUP = PACK * TILES

X_RUNS = ((0, 2), (2, 3))
X_SCALAR = 832
X_CHUNKS = ((1024, 1280), (0, 512), (512, 1024))
RUNS = (3, 3, 2, 2, 2, 1, 1, 1, 1, 1, 1)
SHARES = ((72, 72, 72), (48, 72, 96), (32, 76, 80), (48, 76, 80), (32, 76, 80), (88, 80, 16, 104))
CUT = 60
EARLY = 4
LENT = 32
SCATTERS = ((0, 128), (128, 256), (256, 352), (352, 512))
WARM_UP = (512, 256, 128)
OUT_PIECES = ((0, 256), (256, 608), (608, 992), (992, 1280))


def tile_moe_res_mlp_relu2_kernel(tc, xT, xr, w1, w2, gate, offs, out):
    nc = tc.nc
    with ExitStack() as ctx:
        held = ctx.enter_context(tc.tile_pool(name="held", bufs=1))
        xgrps = ctx.enter_context(tc.tile_pool(name="xgrps", bufs=2))
        wgrps = ctx.enter_context(tc.tile_pool(name="wgrps", bufs=3))
        wcods = ctx.enter_context(tc.tile_pool(name="wcods", bufs=6))
        hids = ctx.enter_context(tc.tile_pool(name="hids", bufs=2))
        psum = ctx.enter_context(tc.psum_pool(name="psum", bufs=1))

        lists = held.tile([P, S // 16], U16, name="lists")
        gate_rows = held.tile([P, C], F32, name="gate_rows")
        nc.vector.memset(gate_rows[:], 0.0)
        planes = held.tile([P, T], U8, name="planes", align_bytes=64)
        nc.vector.memset(planes[:], 0)
        window = held.tile([P, T], F32, name="window")
        nc.vector.memset(window[:], 0.0)
        zeros = held.tile([P, C], F32, name="zeros")
        nc.vector.memset(zeros[:], 0.0)
        gates = held.tile([P, S + LENT], F32, name="gates")
        nc.vector.memset(gates[:, LAST * C : LAST * C + LENT], 1.0)
        identity = held.tile([P, P], F32, name="identity")
        make_identity(nc, identity[:])
        gate_cols = held.tile([P, E], F32, name="gate_cols")
        words = [held.tile([P, T], U32, name=f"words{s}", align_bytes=64) for s in range(PASSES)]
        slot_words = [held.tile([P, S], U32, name=f"slot_words{s}", align_bytes=64) for s in range(PASSES)]
        slot_planes = held.tile([P, S], U8, name="slot_planes", align_bytes=64)
        early_raw = held.tile([P, EARLY * PACK * N], F32, name="early_raw", align_bytes=64)
        w2_raw = {}
        w2_grp = held.tile([P, E * N * PACK], BF16, name="w2_grp", align_bytes=64)
        w2_codes = held.tile([P, E * N], U32, name="w2_codes", align_bytes=64)
        w2_scales = held.tile([P, E * N], U8, name="w2_scales", align_bytes=64)
        last_sums = held.tile([P, 2 * C], F32, name="last_sums")
        result = held.tile([P, T], F32, name="result")
        x_buf = held.tile([P, PASSES * PACK * T], F32, name="x_buf", align_bytes=64)
        x_raw, raw, codes, scales, sums, y_sum, gated, hid, grp, relu = {}, {}, {}, {}, {}, {}, {}, {}, {}, {}

        def load_second(a, b, buf):
            for e in range(a, b):
                w2_raw[e] = buf[:, (e - a) * PACK * N : (e - a + 1) * PACK * N]
            dst = buf[:, : (b - a) * PACK * N].rearrange("p (e q) -> p e q", e=b - a)
            nc.sync.dma_start(out=dst, in_=w2[a:b].rearrange("e (p j) n -> p e (j n)", j=PACK))

        def load_tokens(a, b):
            t = x_buf[:, a * PACK * T : b * PACK * T]
            src = xT[a * K_PASS : b * K_PASS, :].rearrange("(s p j) t -> p s (j t)", s=b - a, j=PACK)
            nc.sync.dma_start(out=t.rearrange("p (s q) -> p s q", s=b - a), in_=src)
            for s in range(a, b):
                x_raw[s] = t[:, (s - a) * PACK * T : (s - a + 1) * PACK * T]

        def load_run(first, count, buf):
            rows = w1.rearrange("e k i -> (e k) i")[first * K_PASS : (first + count) * K_PASS, :]
            for i in range(count):
                raw[first + i] = buf[:, i * WIDE : (i + 1) * WIDE]
            if first + count < E * PASSES:
                dst = buf[:, : count * WIDE].rearrange("p (s q) -> p s q", s=count)
                nc.sync.dma_start(out=dst, in_=rows.rearrange("(s p j) i -> p s (j i)", s=count, j=PACK))
                return
            for m, n in ((0, CUT), (CUT, P)):
                dst = buf[:, m * GROUP : n * GROUP].rearrange("p (j i) -> p j i", j=PACK)
                nc.sync.dma_start(out=dst, in_=rows[:, m * TILES : n * TILES].rearrange("(p j) i -> p j i", j=PACK))

        def spread_gate():
            turned = psum.tile([P, P], F32, name="last0")
            nc.tensor.transpose(turned[:], gate_rows[:], identity[:])
            nc.scalar.activation(gate_cols[:], turned[:, :E], COPY)
            for bank, (a, b) in enumerate(((0, TILES), (TILES, LAST), (LAST, E))):
                wide = psum.tile([P, (b - a) * C], F32, name=f"last{bank + 1}")
                for e in range(a, b):
                    column = gate_cols[:, e : e + 1].to_broadcast([P, P])
                    nc.tensor.transpose(wide[:, (e - a) * C : (e - a + 1) * C], column, identity[:])
                shift = LENT if a == LAST else 0
                nc.scalar.activation(gates[:, a * C + shift : b * C + shift], wide[:], COPY)

        def round_second(e, engine):
            dst = w2_grp[:, e * N * PACK : (e + 1) * N * PACK].rearrange("p (c i j) -> p c j i", i=LINE, j=PACK)
            src = w2_raw[e].rearrange("p (j c i) -> p c j i", i=LINE, j=PACK)
            if engine == "vector":
                nc.vector.tensor_copy(dst, src)
            else:
                nc.scalar.activation(dst, src, COPY)

        def quantise_second(a, b):
            nc.vector.quantize_mx(
                out=w2_codes[:, a * N : b * N].bitcast(FP8X4),
                scales=w2_scales[:, a * N : b * N],
                in_=w2_grp[:, PACK * a * N : PACK * b * N],
            )

        def tokens(s):
            g = xgrps.tile([P, T, PACK], BF16, name="x_grp", align_bytes=64)
            dst = g[:].rearrange("p (c i) j -> p c j i", i=LINE)
            src = x_raw[s].rearrange("p (j c i) -> p c j i", i=LINE, j=PACK)
            first_chunk = X_CHUNKS[1][1]
            for a, b in ((0, first_chunk), (first_chunk, X_SCALAR)):
                nc.scalar.activation(dst[:, a // LINE : b // LINE], src[:, a // LINE : b // LINE], COPY)
            nc.vector.tensor_copy(dst[:, X_SCALAR // LINE :], src[:, X_SCALAR // LINE :])
            flat = g[:].rearrange("p n j -> p (n j)")
            for a, b in X_CHUNKS:
                nc.vector.quantize_mx(
                    out=words[s][:, a:b].bitcast(FP8X4),
                    scales=planes[4 * s : P, a:b],
                    in_=flat[:, PACK * a : PACK * b],
                )
            nc.vector.tensor_copy(slot_words[s][:], words[s][:].indirect(lists[:]))
            if s == PASSES - 1:
                nc.vector.tensor_copy(slot_planes[:], planes[:].indirect(lists[:]))

        def round_pass(e, s):
            g = wgrps.tile([P, H * PACK], BF16, name="w_grp", align_bytes=64)
            grp[e, s] = g
            dst = g[:].rearrange("p (t m j) -> p m j t", t=TILES, j=PACK)
            buf = raw[e * PASSES + s]
            pieces = ((0, P),) if (e, s) != (LAST, PASSES - 1) else ((0, CUT), (CUT, P))
            for (m, n), cut in zip(pieces, SHARES[e][s:]):
                src = buf[:, m * GROUP : n * GROUP].rearrange("p (j m t) -> p m j t", t=TILES, j=PACK)
                mid = P // 2 if m < P // 2 < cut and m else m
                if mid > m:
                    nc.vector.tensor_copy(dst[:, m:mid], src[:, : mid - m])
                nc.vector.tensor_copy(dst[:, mid:cut], src[:, mid - m : cut - m])
                nc.scalar.activation(dst[:, cut:n], src[:, cut - m :], COPY)

        def quantise(e, s):
            c = wcods.tile([P, H], U32, name="w_codes", align_bytes=64)
            z = wcods.tile([P, H], U8, name="w_scales", align_bytes=64)
            codes[e, s], scales[e, s] = c, z
            calls = ((0, H),)
            if (e, s) == (LAST, PASSES - 1):
                calls = [(t * P + h * P // 2, t * P + (h + 1) * P // 2) for h in range(2) for t in range(TILES)]
            for a, b in calls:
                nc.vector.quantize_mx(
                    out=c[:, a:b].bitcast(FP8X4), scales=z[:, a:b], in_=grp[e, s][:, PACK * a : PACK * b]
                )

        def multiply(e, s):
            if s == 0 and e < LAST:
                bank = psum.tile([P, TILES, C], F32, name="sums", bufs=2)
                sums[e] = bank
            elif s == 0:
                sums[e] = [psum.tile([P, C], F32, name=f"last{t}") for t in range(TILES)]
            cols = slice(e * C, (e + 1) * C)
            for t in range(TILES):
                rows = slice(t * P, (t + 1) * P)
                nc.tensor.matmul_mx(
                    out=sums[e][t][:] if e == LAST else sums[e][:, t, :],
                    lhsT=codes[e, s][:, rows].bitcast(FP8X4),
                    lhsT_scale=scales[e, s][:, rows],
                    rhs=slot_words[s][:, cols].bitcast(FP8X4),
                    rhs_scale=slot_planes[4 * s : P, cols],
                    start=(s == 0 and (t == 0 or e == LAST)),
                    stop=(s == PASSES - 1 and (t == TILES - 1 or e == LAST)),
                )

        def warm_up():
            spare = psum.tile([P, H], F32, name="y")
            c, z = codes[LAST, 0], scales[LAST, 0]
            for width in WARM_UP:
                nc.tensor.matmul_mx(
                    out=spare[:, :width],
                    lhsT=c[:, H - P :].bitcast(FP8X4),
                    lhsT_scale=z[:, H - P :],
                    rhs=c[:, :width].bitcast(FP8X4),
                    rhs_scale=z[:, :width],
                    start=True,
                    stop=True,
                )

        def rectify(e):
            if e < LAST:
                r = raw[(e + 1) * PASSES].rearrange("p (j h) -> p j h", j=PACK)[:, :, :C]
                nc.scalar.activation(
                    r.rearrange("p j (c t) -> p j c t", t=TILES),
                    sums[e][:].rearrange("p t (j c) -> p j c t", j=PACK),
                    RELU,
                )
                relu[e] = r
                return
            relu[e] = early_raw[:, : TILES * C]
            for t in range(TILES):
                nc.scalar.activation(relu[e][:, t * C : (t + 1) * C], sums[e][t][:], RELU)

        def square(e):
            if e < LAST:
                if e < LAST - 1:
                    hid[e] = raw[(e + 1) * PASSES + 1][:, : C * TILES // 2].bitcast(BF16)
                else:
                    end = CUT * GROUP + (P // 2 - CUT) * TILES
                    hid[e] = raw[E * PASSES - 1][:, end - C * TILES // 2 : end].bitcast(BF16)
                nc.scalar.activation(hid[e].rearrange("p (j q) -> p j q", j=PACK), relu[e], SQUARE)
                return
            hid[e] = w2_raw[LAST][:, : C * TILES // 2].bitcast(BF16)
            src = relu[e].rearrange("p (t c i) -> p c t i", t=TILES, i=LINE)
            dst = hid[e].rearrange("p (c i t) -> p c t i", i=LINE, t=TILES)
            cut = C // LINE // 2
            nc.vector.tensor_tensor(dst[:, cut:], src[:, cut:], src[:, cut:], MULT)
            nc.scalar.activation(dst[:, :cut], src[:, :cut], SQUARE)

        h_mx = {}

        def quantise_hidden(e):
            c = hids.tile([P, C], U32, name="h_codes", align_bytes=64)
            z = hids.tile([P, C], U8, name="h_scales", align_bytes=64)
            nc.vector.quantize_mx(out=c[:].bitcast(FP8X4), scales=z[:], in_=hid[e])
            h_mx[e] = c, z

        def second_product(e):
            c, z = h_mx[e]
            if e < EARLY:
                y = early_sums[:, e * C : (e + 1) * C]
            else:
                bank = psum.tile([P, C], F32, name="y" if e == LAST else f"last{TILES - 2}")
                y = bank[:]
            cols = slice(e * N, (e + 1) * N)
            nc.tensor.matmul_mx(
                out=y,
                lhsT=w2_codes[:, cols].bitcast(FP8X4),
                lhsT_scale=w2_scales[:, cols],
                rhs=c[:].bitcast(FP8X4),
                rhs_scale=z[:],
                start=True,
                stop=True,
            )
            y_sum[e] = y

        def weigh(e):
            a, b = SCATTERS[e]
            gated[e] = raw[(e + 2) * PASSES - 1][:, : b - a]
            nc.vector.tensor_tensor(gated[e], early_sums[:, a:b], gates[:, a:b], MULT)

        def scatter(e):
            a, b = SCATTERS[e]
            target = window[:].indirect(lists[:, a // 16 : b // 16])
            if e < EARLY - 1:
                nc.vector.tensor_tensor(target, gated[e], zeros[:, : b - a], ADD)
            else:
                nc.scalar.activation(target, gated[e], COPY)

        early_sums = psum.tile([P, EARLY * C], F32, name="early_sums")
        load_second(0, EARLY, early_raw[:])
        nc.sync.dma_start(lists[:], offs)
        nc.sync.dma_start(out=gate_rows[:E, :], in_=gate[0].rearrange("(e c) -> e c", e=E))
        for a, b in X_RUNS:
            load_tokens(a, b)
        starts = [sum(RUNS[:r]) for r in range(len(RUNS))]
        fresh = [held.tile([P, RUNS[r] * WIDE], F32, name=f"fresh{r}", align_bytes=64) for r in range(2)]
        for r in range(2):
            load_run(starts[r], RUNS[r], fresh[r][:])
        for e in range(EARLY):
            round_second(e, "vector" if e % 2 else "scalar")
        quantise_second(0, EARLY)
        spread_gate()
        for s in range(PASSES):
            tokens(s)
        reused = held.tile([P, sum(RUNS[2:5]) * WIDE], F32, name="x_buf", align_bytes=64)
        for r in range(2, 5):
            load_run(starts[r], RUNS[r], reused[:, (starts[r] - starts[2]) * WIDE :])

        for e in range(E):
            round_pass(e, 0)
            if e:
                rectify(e - 1)
            quantise(e, 0)
            multiply(e, 0)
            if e == LAST:
                warm_up()
            round_pass(e, 1)
            if 0 < e < LAST:
                square(e - 1)
            quantise(e, 1)
            if 0 < e < LAST:
                quantise_hidden(e - 1)
            if 0 < e <= EARLY:
                second_product(e - 1)
            multiply(e, 1)
            round_pass(e, 2)
            if e == LAST:
                square(e - 1)
            if 0 < e <= EARLY:
                weigh(e - 1)
            quantise(e, 2)
            multiply(e, 2)
            if 0 < e <= EARLY:
                scatter(e - 1)
            for i in range(e * PASSES, (e + 1) * PASSES):
                if i < len(RUNS) - 5:
                    load_run(starts[5 + i], RUNS[5 + i], raw[i])
                if i == len(RUNS) - 5:
                    load_second(LAST - 1, LAST, raw[i][:, : PACK * N])
                    load_second(LAST, E, raw[i][:, PACK * N :])
                if i == len(RUNS) - 4:
                    residual = raw[i][:, :T]
                    nc.sync.dma_start(out=residual, in_=xr)
        quantise_hidden(LAST - 1)
        round_second(LAST - 1, "scalar")
        round_second(LAST, "vector")
        quantise_second(LAST - 1, LAST)
        quantise_second(LAST, E)
        rectify(LAST)
        second_product(LAST - 1)
        square(LAST)
        a = (LAST - 1) * C
        nc.vector.tensor_tensor(last_sums[:, :C], y_sum[LAST - 1], gates[:, a : a + C], MULT)
        quantise_hidden(LAST)
        second_product(LAST)
        offsets = lists[:, a // 16 : (a + C - LENT) // 16]
        nc.vector.tensor_tensor(window[:].indirect(offsets), last_sums[:, : C - LENT], zeros[:, : C - LENT], ADD)
        nc.scalar.activation(last_sums[:, C:], y_sum[LAST], COPY)
        offsets = lists[:, (LAST * C - LENT) // 16 :]
        nc.vector.tensor_tensor(window[:].indirect(offsets), last_sums[:, C - LENT :], gates[:, LAST * C :], MULT)
        for a, b in OUT_PIECES:
            nc.vector.tensor_tensor(result[:, a:b], window[:, a:b], residual[:, a:b], ADD)
            nc.sync.dma_start(out=out[:, a:b], in_=result[:, a:b])
